import numpy as np
import ml_dtypes


def mxq(x, axis, fmt="e4m3"):
    dtype, down = {"e4m3": (ml_dtypes.float8_e4m3fn, 7), "e5m2": (ml_dtypes.float8_e5m2, 14)}[fmt]
    v = np.moveaxis(np.asarray(x, np.float32).astype(ml_dtypes.bfloat16).astype(np.float64), axis, -1)
    blocks = v.reshape(v.shape[:-1] + (-1, 32))
    amax = np.abs(blocks).max(-1, keepdims=True)
    byte = np.maximum(np.where(amax > 0, np.frexp(amax)[1] - 1 + 127, 0) - down, 1)
    scale = np.exp2(byte - 127.0)
    codes = (blocks / scale).astype(np.float32).astype(dtype).astype(np.float64)
    return np.moveaxis((codes * scale).reshape(v.shape), -1, axis)


WIDE = False


def mx_kscale(k):
    if not WIDE:
        return np.ones(k)
    levels = np.array([24, -24, 12, -12, 0])
    if k % 512:
        return np.exp2(np.random.permutation(np.resize(levels, k // 32))).repeat(32)
    a = np.empty((k // 512, 16))
    for p in range(k // 512):
        a[p, :8] = np.random.permutation(np.resize(levels, 8))
        for g in range(8):
            far = levels[np.abs(levels - a[p, g]) >= 10]
            a[p, g + 8] = far[np.random.randint(len(far))]
    return np.exp2(a.ravel()).repeat(32)


def f64(x):
    return np.asarray(x).astype(np.float64)


def striped8(idx):
    return np.concatenate([v.reshape(-1, 16).T for v in idx]).astype(np.uint16)


def unstriped8(offs):
    return np.stack([offs[16 * g:16 * g + 16].T.reshape(-1) for g in range(8)]).astype(np.int64)


E2M1 = np.array([0.0, 0.5, 1.0, 1.5, 2.0, 3.0, 4.0, 6.0, -0.0, -0.5, -1.0, -1.5, -2.0, -3.0, -4.0, -6.0])


def pack_weight(w, fmt):
    k, n = w.shape
    w = f64(np.asarray(w, np.float32).astype(ml_dtypes.bfloat16)).reshape(k // 32, 32, n)
    amax = np.abs(w).max(1)
    if fmt == "e4m3":
        byte = np.frexp(amax)[1] - 1 + 127 - 7
    else:
        mant, ex = np.frexp(amax / 6.0)
        byte = np.where(mant > 0.5, ex, ex - 1) + 127
    byte = np.clip(np.where(amax > 0, byte, 1), 1, 254)
    scaled = (w * np.exp2(127.0 - byte)[:, None, :]).reshape(k, n).astype(np.float32)
    by_word = np.ascontiguousarray(scaled.reshape(k // 512, 128, 4, n).transpose(0, 1, 3, 2))
    if fmt == "e4m3":
        words = by_word.astype(ml_dtypes.float8_e4m3fn).view(np.uint8)
    else:
        c = by_word.astype(ml_dtypes.float4_e2m1fn).view(np.uint8) & 0xF
        words = (c[..., 0::2] | (c[..., 1::2] << 4)).reshape(k // 512, 128, 2 * n)
    return np.ascontiguousarray(words), np.ascontiguousarray(byte.astype(np.uint8).reshape(k // 512, 16, n))


def unpack_weight(words, scales, fmt):
    g, _, n = scales.shape
    words = np.ascontiguousarray(words).reshape(g, 128, n, -1)
    if fmt == "e4m3":
        vals = words.view(ml_dtypes.float8_e4m3fn).astype(np.float64)
    else:
        nib = np.empty((g, 128, n, 4), np.uint8)
        nib[..., 0::2] = words & 0xF
        nib[..., 1::2] = words >> 4
        vals = E2M1[nib]
    vals = vals * np.repeat(np.exp2(scales.astype(np.float64) - 127.0), 8, axis=1)[..., None]
    return vals.transpose(0, 1, 3, 2).reshape(g * 512, n)


def silu(f):
    return f / (1.0 + np.exp(-np.maximum(f, -700.0)))


K, L, N, T, J = 512, 512, 512, 2048, 1024


def setup_inputs():
    n = np.random.standard_normal
    s = mx_kscale(K)[:, None]
    s2 = mx_kscale(L)[:, None]
    p_wt = pack_weight(n((K, N)) / np.sqrt(K) / s, "e4m3")
    p_wx = pack_weight(n((L, N)) / np.sqrt(L) / s2, "e2m1")
    return {
        "xT": (n((K, T)) * s).astype(np.float32),
        "wgt": np.repeat(np.random.uniform(0.5, 2.0, (8, J)), 16, axis=0).astype(np.float32),
        "wt_words": p_wt[0],
        "wt_scales": p_wt[1],
        "c": (n((L, J)) * s2).astype(np.float32),
        "wx_words": p_wx[0],
        "wx_scales": p_wx[1],
        "b": (0.3 * n(N)).astype(np.float32),
        "offs": striped8(np.stack([np.random.permutation(T)[:J] for _ in range(8)])),
    }


def reference(xT, wgt, wt_words, wt_scales, c, wx_words, wx_scales, b, offs):
    idx = unstriped8(offs)
    rows = np.arange(K)
    xg = f64(wgt)[rows // 4 % 128] * f64(xT)[rows[:, None], idx[rows % 512 // 64]]
    xT_ = mxq(xg, 0, "e4m3")
    wt_ = unpack_weight(wt_words, wt_scales, "e4m3")
    c_q_ = mxq(f64(c), 0, "e4m3")
    c_r_ = mxq(f64(c) - c_q_, 0, "e4m3")
    wx_ = unpack_weight(wx_words, wx_scales, "e2m1")
    y = wt_.T @ xT_ + wx_.T @ c_q_ + wx_.T @ c_r_
    return silu(y + f64(b)[:, None])

@@ -1,0 +1,206 @@
+from contextlib import ExitStack
+
+import concourse.mybir as mybir
+from concourse.masks import make_identity
+
+K, L, N, T, J = 512, 512, 512, 2048, 1024
+FLOPS = 2 * N * J * (K + 2 * L) + 2 * L * L * J
+
+F32 = mybir.dt.float32
+BF16 = mybir.dt.bfloat16
+I32 = mybir.dt.int32
+U32 = mybir.dt.uint32
+U16 = mybir.dt.uint16
+U8 = mybir.dt.uint8
+FP8X4 = mybir.dt.float8_e4m3fn_x4
+FP4X4 = mybir.dt.float4_e2m1fn_x4
+ALU = mybir.AluOpType
+ACT = mybir.ActivationFunctionType
+
+P = 128
+PACK = 4
+SUB = 128
+BANK = 512
+N_TILES = N // P
+C_WIDTHS = (128, 128, 256, 256, 256)
+X_WIDTHS = (256, 256, 256, 128, 128)
+VECTOR_WEAVES = (3, 4)
+
+
+def spans(widths):
+    return [(sum(widths[:q]), sum(widths[: q + 1])) for q in range(len(widths))]
+
+
+def woven(ap):
+    return ap.rearrange("p (c i t) -> p c t i", i=4, t=PACK)
+
+
+def planar(ap):
+    return ap.rearrange("p t (c i) -> p c t i", i=4)
+
+
+def tile_list_silu_kernel(tc, xT, wgt, wt_words, wt_scales, c, wx_words, wx_scales, b, offs, out):
+    nc = tc.nc
+    c_spans = spans(C_WIDTHS)
+    x_spans = spans(X_WIDTHS)
+    with ExitStack() as ctx:
+        keep = ctx.enter_context(tc.tile_pool(name="keep", bufs=1))
+        ring = ctx.enter_context(tc.tile_pool(name="ring", bufs=2))
+        psum = ctx.enter_context(tc.psum_pool(name="psum", bufs=1))
+
+        offsets = keep.tile([P, J // 16], U16, name="offsets")
+        c_f32 = [keep.tile([P, PACK, w], F32, name="c_f32_%d" % q, align_bytes=64) for q, w in enumerate(C_WIDTHS)]
+        planes = [keep.tile([P, T], F32, name="plane_%d" % t, align_bytes=64) for t in range(PACK)]
+        wgt_sb = keep.tile([P, J], F32, name="wgt_sb", align_bytes=64)
+        wt_codes = keep.tile([P, N * 4], U8, name="wt_codes", align_bytes=64)
+        wx_codes = keep.tile([P, N * 2], U8, name="wx_codes", align_bytes=64)
+        wt_plane = keep.tile([P, N], U8, name="wt_plane", align_bytes=64)
+        wx_plane = keep.tile([P, N], U8, name="wx_plane", align_bytes=64)
+        bias = keep.tile([P, N_TILES], F32, name="bias")
+        warm = keep.tile([P, 1], F32, name="warm")
+        warm_out = keep.tile([P, 1], F32, name="warm_out")
+        eye = keep.tile([P, P], BF16, name="eye")
+        eye_bf = keep.tile([P, PACK, P, PACK], BF16, name="eye_bf", align_bytes=64)
+        eye_codes = keep.tile([P, PACK * P], U32, name="eye_codes", align_bytes=64)
+        eye_plane = keep.tile([P, PACK * P], U8, name="eye_plane", align_bytes=64)
+        cq_codes = keep.tile([P, J], U32, name="cq_codes", align_bytes=64)
+        cq_plane = keep.tile([P, J], U8, name="cq_plane", align_bytes=64)
+        cr_codes = keep.tile([P, J], U32, name="cr_codes", align_bytes=64)
+        cr_plane = keep.tile([P, J], U8, name="cr_plane", align_bytes=64)
+        xq_codes = keep.tile([P, J], U32, name="xq_codes", align_bytes=64)
+        xq_plane = keep.tile([P, J], U8, name="xq_plane", align_bytes=64)
+        c_bf = keep.tile([P, J * PACK], BF16, name="c_bf", align_bytes=64)
+        rest_bf = keep.tile([P, J * PACK], BF16, name="rest_bf", align_bytes=64)
+        x_bf = keep.tile([P, J * PACK], BF16, name="x_bf", align_bytes=64)
+
+        nc.gpsimd.memset(warm[:], 0.0)
+        nc.scalar.activation(warm_out[:], warm[:], ACT.Silu)
+        make_identity(nc, eye[:])
+        eye_flat = eye_bf[:].rearrange("p t m i -> p (t m i)")
+        nc.vector.memset(eye_flat.bitcast(I32), 0)
+        for t in range(PACK):
+            nc.vector.tensor_copy(eye_bf[:, t, :, t], eye[:])
+        nc.vector.quantize_mx(out=eye_codes[:].bitcast(FP8X4), scales=eye_plane[:], in_=eye_flat)
+        nc.gpsimd.memset(wx_plane[:].bitcast(I32), 0)
+        nc.gpsimd.memset(wt_plane[:].bitcast(I32), 0)
+
+        c_rows = c.rearrange("(p t) j -> p t j", t=PACK)
+        x_rows = xT.rearrange("(p t) n -> p t n", t=PACK)
+
+        def load_scales(plane, scales, quad):
+            nc.sync.dma_start(plane[32 * quad : 32 * quad + 4, :].bitcast(I32), scales[0, 4 * quad : 4 * quad + 4, :].bitcast(I32))
+
+        for q, (lo, hi) in enumerate(c_spans):
+            nc.sync.dma_start(c_f32[q][:], c_rows[:, :, lo:hi])
+        nc.sync.dma_start(offsets[:], offs)
+        nc.sync.dma_start(wgt_sb[:], wgt)
+        nc.sync.dma_start(planes[0][:], x_rows[:, 0, :])
+        nc.sync.dma_start(planes[1][:], x_rows[:, 1, :])
+        for quad in range(4):
+            load_scales(wx_plane, wx_scales, quad)
+        nc.sync.dma_start(planes[2][:], x_rows[:, 2, :])
+        nc.sync.dma_start(wx_codes[:].bitcast(I32), wx_words[0].bitcast(I32))
+        nc.sync.dma_start(planes[3][:], x_rows[:, 3, :])
+        for quad in range(4):
+            load_scales(wt_plane, wt_scales, quad)
+        nc.sync.dma_start(wt_codes[:].bitcast(I32), wt_words[0].rearrange("p n t -> p (n t)").bitcast(I32))
+        with nc.allow_non_contiguous_dma(reason="one bias value for each partition and tile of output rows"):
+            nc.sync.dma_start(bias[:], b.rearrange("(t p) -> p t", p=P))
+
+        def quantise(codes, plane, source, lo, hi):
+            nc.vector.quantize_mx(out=codes[:, lo:hi].bitcast(FP8X4), scales=plane[:, lo:hi], in_=source[:, lo * PACK : hi * PACK])
+
+        back = {}
+
+        def first_tier(q):
+            lo, hi = c_spans[q]
+            nc.scalar.copy(woven(c_bf[:, lo * PACK : hi * PACK]), planar(c_f32[q][:]))
+            quantise(cq_codes, cq_plane, c_bf, lo, hi)
+            for s0 in range(lo, hi, SUB):
+                bank = psum.tile([P, PACK, SUB], F32, name="back", tag="bank_%d" % (4 + (s0 // SUB) % 4))
+                for t in range(PACK):
+                    nc.tensor.matmul_mx(
+                        out=bank[:, t, :],
+                        lhsT=eye_codes[:, t * P : (t + 1) * P].bitcast(FP8X4), lhsT_scale=eye_plane[:, t * P : (t + 1) * P],
+                        rhs=cq_codes[:, s0 : s0 + SUB].bitcast(FP8X4), rhs_scale=cq_plane[:, s0 : s0 + SUB], start=True, stop=True,
+                    )
+                back[s0] = bank
+
+        def residual(q):
+            lo, hi = c_spans[q]
+            for s0 in range(lo, hi, SUB):
+                nc.vector.tensor_tensor(
+                    woven(rest_bf[:, s0 * PACK : (s0 + SUB) * PACK]),
+                    planar(c_f32[q][:, :, s0 - lo : s0 - lo + SUB]), planar(back[s0][:]), ALU.subtract,
+                )
+
+        first_tier(0)
+        for q in range(len(c_spans)):
+            if q + 1 < len(c_spans):
+                first_tier(q + 1)
+            residual(q)
+            if q > 0:
+                quantise(cr_codes, cr_plane, rest_bf, *c_spans[q - 1])
+        quantise(cr_codes, cr_plane, rest_bf, *c_spans[-1])
+
+        sums, groups = [], []
+        for q, (lo, hi) in enumerate(x_spans):
+            per_bank = BANK // (hi - lo)
+            sums.append([])
+            groups.append([range(u0, u0 + per_bank) for u0 in range(0, N_TILES, per_bank)])
+            for g, tiles in enumerate(groups[q]):
+                bank = psum.tile([P, per_bank, hi - lo], F32, name="sums", tag="bank_%d" % (lo // SUB + g))
+                first = True
+                for u in tiles:
+                    sums[q].append(bank[:, u - tiles[0], :])
+                    n0 = u * P
+                    for codes, plane in ((cq_codes, cq_plane), (cr_codes, cr_plane)):
+                        for s0 in range(lo, hi, SUB):
+                            nc.tensor.matmul_mx(
+                                out=bank[:, u - tiles[0], s0 - lo : s0 - lo + SUB],
+                                lhsT=wx_codes[:, 2 * n0 : 2 * (n0 + P)].bitcast(FP4X4), lhsT_scale=wx_plane[:, n0 : n0 + P],
+                                rhs=codes[:, s0 : s0 + SUB].bitcast(FP8X4), rhs_scale=plane[:, s0 : s0 + SUB], start=first, stop=False,
+                            )
+                            first = False
+
+        picked = {}
+
+        def gather(q):
+            lo, hi = x_spans[q]
+            picked[q] = ring.tile([P, PACK, hi - lo], F32, name="picked", align_bytes=64)
+            for t in range(PACK):
+                nc.vector.tensor_tensor(picked[q][:, t, :], planes[t][:].indirect(offsets[:, lo // 16 : hi // 16]), wgt_sb[:, lo:hi], ALU.mult)
+
+        def weave(q):
+            lo, hi = x_spans[q]
+            if q in VECTOR_WEAVES:
+                nc.vector.tensor_copy(woven(x_bf[:, lo * PACK : hi * PACK]), planar(picked[q][:]))
+            else:
+                nc.scalar.copy(woven(x_bf[:, lo * PACK : hi * PACK]), planar(picked[q][:]))
+
+        out_rows = out.rearrange("(u p) j -> p u j", p=P)
+
+        def finish(q):
+            lo, hi = x_spans[q]
+            quantise(xq_codes, xq_plane, x_bf, lo, hi)
+            for tiles in groups[q]:
+                for u in tiles:
+                    n0 = u * P
+                    nc.tensor.matmul_mx(
+                        out=sums[q][u],
+                        lhsT=wt_codes[:, 4 * n0 : 4 * (n0 + P)].bitcast(FP8X4), lhsT_scale=wt_plane[:, n0 : n0 + P],
+                        rhs=xq_codes[:, lo:hi].bitcast(FP8X4), rhs_scale=xq_plane[:, lo:hi], start=False, stop=(u == tiles[-1]),
+                    )
+            for g, tiles in enumerate(groups[q]):
+                result = keep.tile([P, len(tiles), hi - lo], F32, name="result_%d_%d" % (q, g))
+                for u in tiles:
+                    nc.scalar.activation(result[:, u - tiles[0], :], sums[q][u], ACT.Silu, bias=bias[:, u : u + 1])
+                nc.sync.dma_start(out_rows[:, tiles[0] : tiles[-1] + 1, lo:hi], result[:])
+
+        gather(0)
+        weave(0)
+        for q in range(len(x_spans)):
+            if q + 1 < len(x_spans):
+                gather(q + 1)
+                weave(q + 1)
+            finish(q)

@@ -45,22 +45,21 @@ def tile_list_silu_kernel(tc, xT, wgt, wt_words, wt_scales, c, wx_words, wx_scal
     x_spans = spans(X_WIDTHS)
     with ExitStack() as ctx:
         keep = ctx.enter_context(tc.tile_pool(name="keep", bufs=1))
-        ring = ctx.enter_context(tc.tile_pool(name="ring", bufs=2))
         psum = ctx.enter_context(tc.psum_pool(name="psum", bufs=1))
 
         offsets = keep.tile([P, J // 16], U16, name="offsets")
-        c_f32 = [keep.tile([P, PACK, w], F32, name="c_f32_%d" % q, align_bytes=64) for q, w in enumerate(C_WIDTHS)]
+        c_f32 = [keep.tile([P, PACK, w], F32, name="c_f32", tag="rows_%d" % q, align_bytes=64) for q, w in enumerate(C_WIDTHS)]
         planes = [keep.tile([P, T], F32, name="plane_%d" % t, align_bytes=64) for t in range(PACK)]
         wgt_sb = keep.tile([P, J], F32, name="wgt_sb", align_bytes=64)
         wt_codes = keep.tile([P, N * 4], U8, name="wt_codes", align_bytes=64)
         wx_codes = keep.tile([P, N * 2], U8, name="wx_codes", align_bytes=64)
-        wt_plane = keep.tile([P, N], U8, name="wt_plane", align_bytes=64)
-        wx_plane = keep.tile([P, N], U8, name="wx_plane", align_bytes=64)
+        w_planes = keep.tile([P, 2 * N], U8, name="w_planes", align_bytes=64)
+        wx_plane, wt_plane = w_planes[:, :N], w_planes[:, N:]
         bias = keep.tile([P, N_TILES], F32, name="bias")
         warm = keep.tile([P, 1], F32, name="warm")
         warm_out = keep.tile([P, 1], F32, name="warm_out")
         eye = keep.tile([P, P], BF16, name="eye")
-        eye_bf = keep.tile([P, PACK, P, PACK], BF16, name="eye_bf", align_bytes=64)
+        eye_bf = keep.tile([P, PACK, P, PACK], BF16, name="eye_bf", tag="woven_c", align_bytes=64)
         eye_codes = keep.tile([P, PACK * P], U32, name="eye_codes", align_bytes=64)
         eye_plane = keep.tile([P, PACK * P], U8, name="eye_plane", align_bytes=64)
         cq_codes = keep.tile([P, J], U32, name="cq_codes", align_bytes=64)
@@ -69,11 +68,11 @@ def tile_list_silu_kernel(tc, xT, wgt, wt_words, wt_scales, c, wx_words, wx_scal
         cr_plane = keep.tile([P, J], U8, name="cr_plane", align_bytes=64)
         xq_codes = keep.tile([P, J], U32, name="xq_codes", align_bytes=64)
         xq_plane = keep.tile([P, J], U8, name="xq_plane", align_bytes=64)
-        c_bf = keep.tile([P, J * PACK], BF16, name="c_bf", align_bytes=64)
         rest_bf = keep.tile([P, J * PACK], BF16, name="rest_bf", align_bytes=64)
         x_bf = keep.tile([P, J * PACK], BF16, name="x_bf", align_bytes=64)
 
-        nc.gpsimd.memset(warm[:], 0.0)
+        nc.vector.memset(w_planes[:].bitcast(I32), 0)
+        nc.vector.memset(warm[:], 0.0)
         nc.scalar.activation(warm_out[:], warm[:], ACT.Silu)
         make_identity(nc, eye[:])
         eye_flat = eye_bf[:].rearrange("p t m i -> p (t m i)")
@@ -81,8 +80,7 @@ def tile_list_silu_kernel(tc, xT, wgt, wt_words, wt_scales, c, wx_words, wx_scal
         for t in range(PACK):
             nc.vector.tensor_copy(eye_bf[:, t, :, t], eye[:])
         nc.vector.quantize_mx(out=eye_codes[:].bitcast(FP8X4), scales=eye_plane[:], in_=eye_flat)
-        nc.gpsimd.memset(wx_plane[:].bitcast(I32), 0)
-        nc.gpsimd.memset(wt_plane[:].bitcast(I32), 0)
+        c_bf = keep.tile([P, J * PACK], BF16, name="c_bf", tag="woven_c", align_bytes=64)
 
         c_rows = c.rearrange("(p t) j -> p t j", t=PACK)
         x_rows = xT.rearrange("(p t) n -> p t n", t=PACK)
@@ -93,7 +91,7 @@ def tile_list_silu_kernel(tc, xT, wgt, wt_words, wt_scales, c, wx_words, wx_scal
         for q, (lo, hi) in enumerate(c_spans):
             nc.sync.dma_start(c_f32[q][:], c_rows[:, :, lo:hi])
         nc.sync.dma_start(offsets[:], offs)
-        nc.sync.dma_start(wgt_sb[:], wgt)
+        nc.sync.dma_start(wgt_sb[:, : J // 2], wgt[:, : J // 2])
         nc.sync.dma_start(planes[0][:], x_rows[:, 0, :])
         nc.sync.dma_start(planes[1][:], x_rows[:, 1, :])
         for quad in range(4):
@@ -101,6 +99,7 @@ def tile_list_silu_kernel(tc, xT, wgt, wt_words, wt_scales, c, wx_words, wx_scal
         nc.sync.dma_start(planes[2][:], x_rows[:, 2, :])
         nc.sync.dma_start(wx_codes[:].bitcast(I32), wx_words[0].bitcast(I32))
         nc.sync.dma_start(planes[3][:], x_rows[:, 3, :])
+        nc.sync.dma_start(wgt_sb[:, J // 2 :], wgt[:, J // 2 :])
         for quad in range(4):
             load_scales(wt_plane, wt_scales, quad)
         nc.sync.dma_start(wt_codes[:].bitcast(I32), wt_words[0].rearrange("p n t -> p (n t)").bitcast(I32))
@@ -114,10 +113,13 @@ def tile_list_silu_kernel(tc, xT, wgt, wt_words, wt_scales, c, wx_words, wx_scal
 
         def first_tier(q):
             lo, hi = c_spans[q]
-            nc.scalar.copy(woven(c_bf[:, lo * PACK : hi * PACK]), planar(c_f32[q][:]))
+            if q == 0:
+                nc.vector.tensor_copy(woven(c_bf[:, lo * PACK : hi * PACK]), planar(c_f32[q][:]))
+            else:
+                nc.scalar.copy(woven(c_bf[:, lo * PACK : hi * PACK]), planar(c_f32[q][:]))
             quantise(cq_codes, cq_plane, c_bf, lo, hi)
             for s0 in range(lo, hi, SUB):
-                bank = psum.tile([P, PACK, SUB], F32, name="back", tag="bank_%d" % (4 + (s0 // SUB) % 4))
+                bank = psum.tile([P, PACK, SUB], F32, name="back", tag="bank_%d" % (s0 // SUB))
                 for t in range(PACK):
                     nc.tensor.matmul_mx(
                         out=bank[:, t, :],
@@ -139,9 +141,9 @@ def tile_list_silu_kernel(tc, xT, wgt, wt_words, wt_scales, c, wx_words, wx_scal
             if q + 1 < len(c_spans):
                 first_tier(q + 1)
             residual(q)
-            if q > 0:
-                quantise(cr_codes, cr_plane, rest_bf, *c_spans[q - 1])
-        quantise(cr_codes, cr_plane, rest_bf, *c_spans[-1])
+            if c_spans[q][0] == J // 2:
+                quantise(cr_codes, cr_plane, rest_bf, 0, J // 2)
+        quantise(cr_codes, cr_plane, rest_bf, J // 2, J)
 
         sums, groups = [], []
         for q, (lo, hi) in enumerate(x_spans):
@@ -149,7 +151,7 @@ def tile_list_silu_kernel(tc, xT, wgt, wt_words, wt_scales, c, wx_words, wx_scal
             sums.append([])
             groups.append([range(u0, u0 + per_bank) for u0 in range(0, N_TILES, per_bank)])
             for g, tiles in enumerate(groups[q]):
-                bank = psum.tile([P, per_bank, hi - lo], F32, name="sums", tag="bank_%d" % (lo // SUB + g))
+                bank = psum.tile([P, per_bank, hi - lo], F32, name="sums", tag="bank_%d" % (J // SUB - 1 - lo // SUB - g))
                 first = True
                 for u in tiles:
                     sums[q].append(bank[:, u - tiles[0], :])
@@ -165,11 +167,14 @@ def tile_list_silu_kernel(tc, xT, wgt, wt_words, wt_scales, c, wx_words, wx_scal
 
         picked = {}
 
-        def gather(q):
-            lo, hi = x_spans[q]
-            picked[q] = ring.tile([P, PACK, hi - lo], F32, name="picked", align_bytes=64)
+        def gather(chunks):
+            for q in chunks:
+                lo, hi = x_spans[q]
+                picked[q] = keep.tile([P, PACK, hi - lo], F32, name="picked", tag="rows_%d" % (len(c_spans) - 1 - q % 2), align_bytes=64)
             for t in range(PACK):
-                nc.vector.tensor_tensor(picked[q][:, t, :], planes[t][:].indirect(offsets[:, lo // 16 : hi // 16]), wgt_sb[:, lo:hi], ALU.mult)
+                for q in chunks:
+                    lo, hi = x_spans[q]
+                    nc.vector.tensor_tensor(picked[q][:, t, :], planes[t][:].indirect(offsets[:, lo // 16 : hi // 16]), wgt_sb[:, lo:hi], ALU.mult)
 
         def weave(q):
             lo, hi = x_spans[q]
@@ -197,10 +202,11 @@ def tile_list_silu_kernel(tc, xT, wgt, wt_words, wt_scales, c, wx_words, wx_scal
                     nc.scalar.activation(result[:, u - tiles[0], :], sums[q][u], ACT.Silu, bias=bias[:, u : u + 1])
                 nc.sync.dma_start(out_rows[:, tiles[0] : tiles[-1] + 1, lo:hi], result[:])
 
-        gather(0)
+        gather((0, 1))
         weave(0)
         for q in range(len(x_spans)):
             if q + 1 < len(x_spans):
-                gather(q + 1)
                 weave(q + 1)
             finish(q)
+            if q + 2 < len(x_spans):
+                gather((q + 2,))

@@ -23,8 +23,11 @@ SUB = 128
 BANK = 512
 N_TILES = N // P
 C_WIDTHS = (128, 128, 256, 256, 256)
+T_WIDTHS = (128, 128, 128, 128, 256, 256)
+VECTOR_TIERS = (0, 2)
 X_WIDTHS = (256, 256, 256, 128, 128)
-VECTOR_WEAVES = (3, 4)
+EARLY_CHUNKS = 3
+EARLY = sum(X_WIDTHS[:EARLY_CHUNKS])
 
 
 def spans(widths):
@@ -32,16 +35,17 @@ def spans(widths):
 
 
 def woven(ap):
-    return ap.rearrange("p (c i t) -> p c t i", i=4, t=PACK)
+    return ap.rearrange("p (c i t) -> p c t i", i=2, t=PACK)
 
 
 def planar(ap):
-    return ap.rearrange("p t (c i) -> p c t i", i=4)
+    return ap.rearrange("p t (c i) -> p c t i", i=2)
 
 
 def tile_list_silu_kernel(tc, xT, wgt, wt_words, wt_scales, c, wx_words, wx_scales, b, offs, out):
     nc = tc.nc
     c_spans = spans(C_WIDTHS)
+    t_spans = spans(T_WIDTHS)
     x_spans = spans(X_WIDTHS)
     with ExitStack() as ctx:
         keep = ctx.enter_context(tc.tile_pool(name="keep", bufs=1))
@@ -59,7 +63,7 @@ def tile_list_silu_kernel(tc, xT, wgt, wt_words, wt_scales, c, wx_words, wx_scal
         warm = keep.tile([P, 1], F32, name="warm")
         warm_out = keep.tile([P, 1], F32, name="warm_out")
         eye = keep.tile([P, P], BF16, name="eye")
-        eye_bf = keep.tile([P, PACK, P, PACK], BF16, name="eye_bf", tag="woven_c", align_bytes=64)
+        eye_bf = keep.tile([P, PACK * (PACK * P + 1)], BF16, name="eye_bf", tag="woven_c", align_bytes=64)
         eye_codes = keep.tile([P, PACK * P], U32, name="eye_codes", align_bytes=64)
         eye_plane = keep.tile([P, PACK * P], U8, name="eye_plane", align_bytes=64)
         cq_codes = keep.tile([P, J], U32, name="cq_codes", align_bytes=64)
@@ -69,17 +73,15 @@ def tile_list_silu_kernel(tc, xT, wgt, wt_words, wt_scales, c, wx_words, wx_scal
         xq_codes = keep.tile([P, J], U32, name="xq_codes", align_bytes=64)
         xq_plane = keep.tile([P, J], U8, name="xq_plane", align_bytes=64)
         rest_bf = keep.tile([P, J * PACK], BF16, name="rest_bf", align_bytes=64)
-        x_bf = keep.tile([P, J * PACK], BF16, name="x_bf", align_bytes=64)
 
-        nc.vector.memset(w_planes[:].bitcast(I32), 0)
+        make_identity(nc, eye[:])
         nc.vector.memset(warm[:], 0.0)
         nc.scalar.activation(warm_out[:], warm[:], ACT.Silu)
-        make_identity(nc, eye[:])
-        eye_flat = eye_bf[:].rearrange("p t m i -> p (t m i)")
-        nc.vector.memset(eye_flat.bitcast(I32), 0)
-        for t in range(PACK):
-            nc.vector.tensor_copy(eye_bf[:, t, :, t], eye[:])
-        nc.vector.quantize_mx(out=eye_codes[:].bitcast(FP8X4), scales=eye_plane[:], in_=eye_flat)
+        nc.vector.memset(eye_bf[:].bitcast(I32), 0)
+        nc.vector.memset(w_planes[:].bitcast(I32), 0)
+        diagonal = eye_bf[:].rearrange("p (t r) -> p t r", t=PACK)[:, :, 0 : PACK * P : PACK]
+        nc.vector.tensor_copy(diagonal, eye[:].unsqueeze(1).to_broadcast([P, PACK, P]))
+        nc.vector.quantize_mx(out=eye_codes[:].bitcast(FP8X4), scales=eye_plane[:], in_=eye_bf[:, : PACK * PACK * P])
         c_bf = keep.tile([P, J * PACK], BF16, name="c_bf", tag="woven_c", align_bytes=64)
 
         c_rows = c.rearrange("(p t) j -> p t j", t=PACK)
@@ -91,7 +93,7 @@ def tile_list_silu_kernel(tc, xT, wgt, wt_words, wt_scales, c, wx_words, wx_scal
         for q, (lo, hi) in enumerate(c_spans):
             nc.sync.dma_start(c_f32[q][:], c_rows[:, :, lo:hi])
         nc.sync.dma_start(offsets[:], offs)
-        nc.sync.dma_start(wgt_sb[:, : J // 2], wgt[:, : J // 2])
+        nc.sync.dma_start(wgt_sb[:, :EARLY], wgt[:, :EARLY])
         nc.sync.dma_start(planes[0][:], x_rows[:, 0, :])
         nc.sync.dma_start(planes[1][:], x_rows[:, 1, :])
         for quad in range(4):
@@ -99,25 +101,31 @@ def tile_list_silu_kernel(tc, xT, wgt, wt_words, wt_scales, c, wx_words, wx_scal
         nc.sync.dma_start(planes[2][:], x_rows[:, 2, :])
         nc.sync.dma_start(wx_codes[:].bitcast(I32), wx_words[0].bitcast(I32))
         nc.sync.dma_start(planes[3][:], x_rows[:, 3, :])
-        nc.sync.dma_start(wgt_sb[:, J // 2 :], wgt[:, J // 2 :])
         for quad in range(4):
             load_scales(wt_plane, wt_scales, quad)
         nc.sync.dma_start(wt_codes[:].bitcast(I32), wt_words[0].rearrange("p n t -> p (n t)").bitcast(I32))
         with nc.allow_non_contiguous_dma(reason="one bias value for each partition and tile of output rows"):
             nc.sync.dma_start(bias[:], b.rearrange("(t p) -> p t", p=P))
+        nc.sync.dma_start(wgt_sb[:, EARLY:], wgt[:, EARLY:])
 
         def quantise(codes, plane, source, lo, hi):
             nc.vector.quantize_mx(out=codes[:, lo:hi].bitcast(FP8X4), scales=plane[:, lo:hi], in_=source[:, lo * PACK : hi * PACK])
 
         back = {}
 
+        def c_columns(lo, hi):
+            q = max(q for q, span in enumerate(c_spans) if span[0] <= lo)
+            return c_f32[q][:, :, lo - c_spans[q][0] : hi - c_spans[q][0]]
+
         def first_tier(q):
-            lo, hi = c_spans[q]
-            if q == 0:
-                nc.vector.tensor_copy(woven(c_bf[:, lo * PACK : hi * PACK]), planar(c_f32[q][:]))
+            lo, hi = t_spans[q]
+            if q in VECTOR_TIERS:
+                part = c_bf[:, : (hi - lo) * PACK]
+                nc.vector.tensor_copy(woven(part), planar(c_columns(lo, hi)))
             else:
-                nc.scalar.copy(woven(c_bf[:, lo * PACK : hi * PACK]), planar(c_f32[q][:]))
-            quantise(cq_codes, cq_plane, c_bf, lo, hi)
+                part = c_bf[:, lo * PACK : hi * PACK]
+                nc.scalar.copy(woven(part), planar(c_columns(lo, hi)))
+            nc.vector.quantize_mx(out=cq_codes[:, lo:hi].bitcast(FP8X4), scales=cq_plane[:, lo:hi], in_=part)
             for s0 in range(lo, hi, SUB):
                 bank = psum.tile([P, PACK, SUB], F32, name="back", tag="bank_%d" % (s0 // SUB))
                 for t in range(PACK):
@@ -129,19 +137,20 @@ def tile_list_silu_kernel(tc, xT, wgt, wt_words, wt_scales, c, wx_words, wx_scal
                 back[s0] = bank
 
         def residual(q):
-            lo, hi = c_spans[q]
+            lo, hi = t_spans[q]
             for s0 in range(lo, hi, SUB):
                 nc.vector.tensor_tensor(
                     woven(rest_bf[:, s0 * PACK : (s0 + SUB) * PACK]),
-                    planar(c_f32[q][:, :, s0 - lo : s0 - lo + SUB]), planar(back[s0][:]), ALU.subtract,
+                    planar(c_columns(s0, s0 + SUB)), planar(back[s0][:]), ALU.subtract,
                 )
 
         first_tier(0)
-        for q in range(len(c_spans)):
-            if q + 1 < len(c_spans):
-                first_tier(q + 1)
+        first_tier(1)
+        for q in range(len(t_spans)):
+            if q + 2 < len(t_spans):
+                first_tier(q + 2)
             residual(q)
-            if c_spans[q][0] == J // 2:
+            if t_spans[q][0] == J // 2:
                 quantise(cr_codes, cr_plane, rest_bf, 0, J // 2)
         quantise(cr_codes, cr_plane, rest_bf, J // 2, J)
 
@@ -165,29 +174,16 @@ def tile_list_silu_kernel(tc, xT, wgt, wt_words, wt_scales, c, wx_words, wx_scal
                             )
                             first = False
 
-        picked = {}
+        x_bf = [keep.tile([P, w * PACK], BF16, name="x_bf", tag="woven_x_%d" % q, align_bytes=64) for q, w in enumerate(X_WIDTHS)]
 
-        def gather(chunks):
-            for q in chunks:
-                lo, hi = x_spans[q]
-                picked[q] = keep.tile([P, PACK, hi - lo], F32, name="picked", tag="rows_%d" % (len(c_spans) - 1 - q % 2), align_bytes=64)
-            for t in range(PACK):
-                for q in chunks:
-                    lo, hi = x_spans[q]
-                    nc.vector.tensor_tensor(picked[q][:, t, :], planes[t][:].indirect(offsets[:, lo // 16 : hi // 16]), wgt_sb[:, lo:hi], ALU.mult)
-
-        def weave(q):
-            lo, hi = x_spans[q]
-            if q in VECTOR_WEAVES:
-                nc.vector.tensor_copy(woven(x_bf[:, lo * PACK : hi * PACK]), planar(picked[q][:]))
-            else:
-                nc.scalar.copy(woven(x_bf[:, lo * PACK : hi * PACK]), planar(picked[q][:]))
+        def gather(dst, t, lo, hi):
+            nc.vector.tensor_tensor(dst, planes[t][:].indirect(offsets[:, lo // 16 : hi // 16]), wgt_sb[:, lo:hi], ALU.mult)
 
         out_rows = out.rearrange("(u p) j -> p u j", p=P)
 
         def finish(q):
             lo, hi = x_spans[q]
-            quantise(xq_codes, xq_plane, x_bf, lo, hi)
+            nc.vector.quantize_mx(out=xq_codes[:, lo:hi].bitcast(FP8X4), scales=xq_plane[:, lo:hi], in_=x_bf[q][:])
             for tiles in groups[q]:
                 for u in tiles:
                     n0 = u * P
@@ -196,17 +192,33 @@ def tile_list_silu_kernel(tc, xT, wgt, wt_words, wt_scales, c, wx_words, wx_scal
                         lhsT=wt_codes[:, 4 * n0 : 4 * (n0 + P)].bitcast(FP8X4), lhsT_scale=wt_plane[:, n0 : n0 + P],
                         rhs=xq_codes[:, lo:hi].bitcast(FP8X4), rhs_scale=xq_plane[:, lo:hi], start=False, stop=(u == tiles[-1]),
                     )
-            for g, tiles in enumerate(groups[q]):
+            for g, tiles in enumerate((range(0, 2), range(2, 4))):
                 result = keep.tile([P, len(tiles), hi - lo], F32, name="result_%d_%d" % (q, g))
                 for u in tiles:
                     nc.scalar.activation(result[:, u - tiles[0], :], sums[q][u], ACT.Silu, bias=bias[:, u : u + 1])
                 nc.sync.dma_start(out_rows[:, tiles[0] : tiles[-1] + 1, lo:hi], result[:])
 
-        gather((0, 1))
-        weave(0)
-        for q in range(len(x_spans)):
-            if q + 1 < len(x_spans):
-                weave(q + 1)
+        early = keep.tile([P, PACK, EARLY], F32, name="early", tag="rows_%d" % (len(c_spans) - 1), align_bytes=64)
+
+        def weave_pair(q, t):
+            lo, hi = x_spans[q]
+            nc.scalar.copy(woven(x_bf[q][:])[:, :, t : t + 2, :], planar(early[:, t : t + 2, lo:hi]))
+
+        for t in range(PACK - 1):
+            gather(early[:, t, :], t, 0, EARLY)
+            if t == 1:
+                for q in range(EARLY_CHUNKS):
+                    weave_pair(q, 0)
+        for q in range(EARLY_CHUNKS):
+            lo, hi = x_spans[q]
+            gather(early[:, PACK - 1, lo:hi], PACK - 1, lo, hi)
+            weave_pair(q, 2)
+        for q in range(EARLY_CHUNKS):
             finish(q)
-            if q + 2 < len(x_spans):
-                gather((q + 2,))
+        for q in range(EARLY_CHUNKS, len(x_spans)):
+            lo, hi = x_spans[q]
+            late = keep.tile([P, PACK, hi - lo], F32, name="late", tag="woven_x_%d" % (q - 2), align_bytes=64)
+            for t in range(PACK):
+                gather(late[:, t, :], t, lo, hi)
+            nc.vector.tensor_copy(woven(x_bf[q][:]), planar(late[:]))
+            finish(q)

@@ -25,9 +25,8 @@ N_TILES = N // P
 C_WIDTHS = (128, 128, 256, 256, 256)
 T_WIDTHS = (128, 128, 128, 128, 256, 256)
 VECTOR_TIERS = (0, 2)
-X_WIDTHS = (256, 256, 256, 128, 128)
-EARLY_CHUNKS = 3
-EARLY = sum(X_WIDTHS[:EARLY_CHUNKS])
+X_WIDTHS = (128, 256, 256, 256, 128)
+EARLY = J - X_WIDTHS[-1]
 
 
 def spans(widths):
@@ -95,18 +94,18 @@ def tile_list_silu_kernel(tc, xT, wgt, wt_words, wt_scales, c, wx_words, wx_scal
         nc.sync.dma_start(offsets[:], offs)
         nc.sync.dma_start(wgt_sb[:, :EARLY], wgt[:, :EARLY])
         nc.sync.dma_start(planes[0][:], x_rows[:, 0, :])
-        nc.sync.dma_start(planes[1][:], x_rows[:, 1, :])
+        nc.sync.dma_start(wx_codes[:].bitcast(I32), wx_words[0].bitcast(I32))
         for quad in range(4):
             load_scales(wx_plane, wx_scales, quad)
-        nc.sync.dma_start(planes[2][:], x_rows[:, 2, :])
-        nc.sync.dma_start(wx_codes[:].bitcast(I32), wx_words[0].bitcast(I32))
-        nc.sync.dma_start(planes[3][:], x_rows[:, 3, :])
+        nc.sync.dma_start(planes[1][:], x_rows[:, 1, :])
         for quad in range(4):
             load_scales(wt_plane, wt_scales, quad)
+        nc.sync.dma_start(planes[2][:], x_rows[:, 2, :])
+        nc.sync.dma_start(planes[3][:], x_rows[:, 3, :])
         nc.sync.dma_start(wt_codes[:].bitcast(I32), wt_words[0].rearrange("p n t -> p (n t)").bitcast(I32))
+        nc.sync.dma_start(wgt_sb[:, EARLY:], wgt[:, EARLY:])
         with nc.allow_non_contiguous_dma(reason="one bias value for each partition and tile of output rows"):
             nc.sync.dma_start(bias[:], b.rearrange("(t p) -> p t", p=P))
-        nc.sync.dma_start(wgt_sb[:, EARLY:], wgt[:, EARLY:])
 
         def quantise(codes, plane, source, lo, hi):
             nc.vector.quantize_mx(out=codes[:, lo:hi].bitcast(FP8X4), scales=plane[:, lo:hi], in_=source[:, lo * PACK : hi * PACK])
@@ -200,25 +199,46 @@ def tile_list_silu_kernel(tc, xT, wgt, wt_words, wt_scales, c, wx_words, wx_scal
 
         early = keep.tile([P, PACK, EARLY], F32, name="early", tag="rows_%d" % (len(c_spans) - 1), align_bytes=64)
 
-        def weave_pair(q, t):
+        def weave_pair(q, t, engine_copy):
             lo, hi = x_spans[q]
-            nc.scalar.copy(woven(x_bf[q][:])[:, :, t : t + 2, :], planar(early[:, t : t + 2, lo:hi]))
+            engine_copy(woven(x_bf[q][:])[:, :, t : t + 2, :], planar(early[:, t : t + 2, lo:hi]))
 
-        for t in range(PACK - 1):
-            gather(early[:, t, :], t, 0, EARLY)
-            if t == 1:
-                for q in range(EARLY_CHUNKS):
-                    weave_pair(q, 0)
-        for q in range(EARLY_CHUNKS):
+        def last_plane(q):
             lo, hi = x_spans[q]
             gather(early[:, PACK - 1, lo:hi], PACK - 1, lo, hi)
-            weave_pair(q, 2)
-        for q in range(EARLY_CHUNKS):
-            finish(q)
-        for q in range(EARLY_CHUNKS, len(x_spans)):
-            lo, hi = x_spans[q]
-            late = keep.tile([P, PACK, hi - lo], F32, name="late", tag="woven_x_%d" % (q - 2), align_bytes=64)
-            for t in range(PACK):
-                gather(late[:, t, :], t, lo, hi)
-            nc.vector.tensor_copy(woven(x_bf[q][:]), planar(late[:]))
-            finish(q)
+
+        last = len(x_spans) - 1
+
+        late = keep.tile([P, PACK, J - EARLY], F32, name="late", align_bytes=64)
+
+        def late_plane(t):
+            gather(late[:, t, :], t, EARLY, J)
+
+        gather(early[:, 0, :EARLY], 0, 0, EARLY)
+        split = x_spans[1][1]
+        gather(early[:, 1, :split], 1, 0, split)
+        for q in range(2):
+            weave_pair(q, 0, nc.scalar.copy)
+        gather(early[:, 1, split:EARLY], 1, split, EARLY)
+        for q in range(2, last):
+            weave_pair(q, 0, nc.scalar.copy)
+        gather(early[:, 2, :EARLY], 2, 0, EARLY)
+
+        last_plane(0)
+        weave_pair(0, 2, nc.scalar.copy)
+        last_plane(1)
+        finish(0)
+        weave_pair(1, 2, nc.vector.tensor_copy)
+        last_plane(2)
+        finish(1)
+        weave_pair(2, 2, nc.vector.tensor_copy)
+        last_plane(3)
+        finish(2)
+        late_plane(0)
+        weave_pair(3, 2, nc.vector.tensor_copy)
+        late_plane(1)
+        finish(3)
+        late_plane(2)
+        late_plane(3)
+        nc.vector.tensor_copy(woven(x_bf[last][:]), planar(late[:]))
+        finish(last)

@@ -22,11 +22,15 @@ PACK = 4
 SUB = 128
 BANK = 512
 N_TILES = N // P
+HALF = J // 2
 C_WIDTHS = (128, 128, 256, 256, 256)
+EARLY_LOADS = 4
 T_WIDTHS = (128, 128, 128, 128, 256, 256)
-VECTOR_TIERS = (0, 2)
-X_WIDTHS = (128, 256, 256, 256, 128)
-EARLY = J - X_WIDTHS[-1]
+EARLY_TIERS = 5
+EARLY = 768
+VECTOR_TIERS = (0, 2, 5)
+X_WIDTHS = (256, 256, 256, 256)
+LATE_WIDTHS = (256, 128, 128)
 
 
 def spans(widths):
@@ -71,7 +75,7 @@ def tile_list_silu_kernel(tc, xT, wgt, wt_words, wt_scales, c, wx_words, wx_scal
         cr_plane = keep.tile([P, J], U8, name="cr_plane", align_bytes=64)
         xq_codes = keep.tile([P, J], U32, name="xq_codes", align_bytes=64)
         xq_plane = keep.tile([P, J], U8, name="xq_plane", align_bytes=64)
-        rest_bf = keep.tile([P, J * PACK], BF16, name="rest_bf", align_bytes=64)
+        rest_bf = keep.tile([P, EARLY * PACK], BF16, name="rest_bf", align_bytes=64)
 
         make_identity(nc, eye[:])
         nc.vector.memset(warm[:], 0.0)
@@ -83,27 +87,35 @@ def tile_list_silu_kernel(tc, xT, wgt, wt_words, wt_scales, c, wx_words, wx_scal
         nc.vector.quantize_mx(out=eye_codes[:].bitcast(FP8X4), scales=eye_plane[:], in_=eye_bf[:, : PACK * PACK * P])
         c_bf = keep.tile([P, J * PACK], BF16, name="c_bf", tag="woven_c", align_bytes=64)
 
+        late_c_bf = keep.tile([P, (J - EARLY) * PACK], BF16, name="late_c_bf", tag="late", align_bytes=64)
+
         c_rows = c.rearrange("(p t) j -> p t j", t=PACK)
         x_rows = xT.rearrange("(p t) n -> p t n", t=PACK)
 
         def load_scales(plane, scales, quad):
             nc.sync.dma_start(plane[32 * quad : 32 * quad + 4, :].bitcast(I32), scales[0, 4 * quad : 4 * quad + 4, :].bitcast(I32))
 
-        for q, (lo, hi) in enumerate(c_spans):
+        def load_c(q):
+            lo, hi = c_spans[q]
             nc.sync.dma_start(c_f32[q][:], c_rows[:, :, lo:hi])
+
+        for q in range(EARLY_LOADS):
+            load_c(q)
         nc.sync.dma_start(offsets[:], offs)
-        nc.sync.dma_start(wgt_sb[:, :EARLY], wgt[:, :EARLY])
+        nc.sync.dma_start(wgt_sb[:, :HALF], wgt[:, :HALF])
         nc.sync.dma_start(planes[0][:], x_rows[:, 0, :])
-        nc.sync.dma_start(wx_codes[:].bitcast(I32), wx_words[0].bitcast(I32))
-        for quad in range(4):
-            load_scales(wx_plane, wx_scales, quad)
+        nc.sync.dma_start(wgt_sb[:, HALF:], wgt[:, HALF:])
         nc.sync.dma_start(planes[1][:], x_rows[:, 1, :])
         for quad in range(4):
-            load_scales(wt_plane, wt_scales, quad)
+            load_scales(wx_plane, wx_scales, quad)
         nc.sync.dma_start(planes[2][:], x_rows[:, 2, :])
+        for quad in range(4):
+            load_scales(wt_plane, wt_scales, quad)
+        nc.sync.dma_start(wx_codes[:].bitcast(I32), wx_words[0].bitcast(I32))
         nc.sync.dma_start(planes[3][:], x_rows[:, 3, :])
         nc.sync.dma_start(wt_codes[:].bitcast(I32), wt_words[0].rearrange("p n t -> p (n t)").bitcast(I32))
-        nc.sync.dma_start(wgt_sb[:, EARLY:], wgt[:, EARLY:])
+        for q in range(EARLY_LOADS, len(c_spans)):
+            load_c(q)
         with nc.allow_non_contiguous_dma(reason="one bias value for each partition and tile of output rows"):
             nc.sync.dma_start(bias[:], b.rearrange("(t p) -> p t", p=P))
 
@@ -116,15 +128,22 @@ def tile_list_silu_kernel(tc, xT, wgt, wt_words, wt_scales, c, wx_words, wx_scal
             q = max(q for q, span in enumerate(c_spans) if span[0] <= lo)
             return c_f32[q][:, :, lo - c_spans[q][0] : hi - c_spans[q][0]]
 
+        def tier_part(q):
+            lo, hi = t_spans[q]
+            if q in (0, 2):
+                return c_bf[:, : (hi - lo) * PACK]
+            if q == EARLY_TIERS:
+                return late_c_bf[:]
+            return c_bf[:, lo * PACK : hi * PACK]
+
+        def weave_c(q):
+            lo, hi = t_spans[q]
+            copy = nc.vector.tensor_copy if q in VECTOR_TIERS else nc.scalar.copy
+            copy(woven(tier_part(q)), planar(c_columns(lo, hi)))
+
         def first_tier(q):
             lo, hi = t_spans[q]
-            if q in VECTOR_TIERS:
-                part = c_bf[:, : (hi - lo) * PACK]
-                nc.vector.tensor_copy(woven(part), planar(c_columns(lo, hi)))
-            else:
-                part = c_bf[:, lo * PACK : hi * PACK]
-                nc.scalar.copy(woven(part), planar(c_columns(lo, hi)))
-            nc.vector.quantize_mx(out=cq_codes[:, lo:hi].bitcast(FP8X4), scales=cq_plane[:, lo:hi], in_=part)
+            nc.vector.quantize_mx(out=cq_codes[:, lo:hi].bitcast(FP8X4), scales=cq_plane[:, lo:hi], in_=tier_part(q))
             for s0 in range(lo, hi, SUB):
                 bank = psum.tile([P, PACK, SUB], F32, name="back", tag="bank_%d" % (s0 // SUB))
                 for t in range(PACK):
@@ -135,110 +154,135 @@ def tile_list_silu_kernel(tc, xT, wgt, wt_words, wt_scales, c, wx_words, wx_scal
                     )
                 back[s0] = bank
 
-        def residual(q):
-            lo, hi = t_spans[q]
-            for s0 in range(lo, hi, SUB):
-                nc.vector.tensor_tensor(
-                    woven(rest_bf[:, s0 * PACK : (s0 + SUB) * PACK]),
-                    planar(c_columns(s0, s0 + SUB)), planar(back[s0][:]), ALU.subtract,
-                )
+        def residual(s0, dst=None):
+            dst = rest_bf[:, s0 * PACK : (s0 + SUB) * PACK] if dst is None else dst
+            nc.vector.tensor_tensor(
+                woven(dst),
+                planar(c_columns(s0, s0 + SUB)), planar(back[s0][:]), ALU.subtract,
+            )
 
-        first_tier(0)
-        first_tier(1)
-        for q in range(len(t_spans)):
-            if q + 2 < len(t_spans):
+        def wx_pass(dst, u, codes, plane, lo, hi, start, stop):
+            n0 = u * P
+            nc.tensor.matmul_mx(
+                out=dst, lhsT=wx_codes[:, 2 * n0 : 2 * (n0 + P)].bitcast(FP4X4), lhsT_scale=wx_plane[:, n0 : n0 + P],
+                rhs=codes[:, lo:hi].bitcast(FP8X4), rhs_scale=plane[:, lo:hi], start=start, stop=stop,
+            )
+
+        def wt_pass(dst, u, lo, hi, start, stop):
+            n0 = u * P
+            nc.tensor.matmul_mx(
+                out=dst, lhsT=wt_codes[:, 4 * n0 : 4 * (n0 + P)].bitcast(FP8X4), lhsT_scale=wt_plane[:, n0 : n0 + P],
+                rhs=xq_codes[:, lo:hi].bitcast(FP8X4), rhs_scale=xq_plane[:, lo:hi], start=start, stop=stop,
+            )
+
+        for q in range(2):
+            weave_c(q)
+            first_tier(q)
+        for q in range(EARLY_TIERS):
+            if q + 2 < EARLY_TIERS:
+                weave_c(q + 2)
                 first_tier(q + 2)
-            residual(q)
-            if t_spans[q][0] == J // 2:
-                quantise(cr_codes, cr_plane, rest_bf, 0, J // 2)
-        quantise(cr_codes, cr_plane, rest_bf, J // 2, J)
+            for s0 in range(t_spans[q][0], t_spans[q][1], SUB):
+                residual(s0)
+            if t_spans[q][0] == HALF:
+                quantise(cr_codes, cr_plane, rest_bf, 0, HALF)
+        quantise(cr_codes, cr_plane, rest_bf, HALF, EARLY)
 
-        sums, groups = [], []
-        for q, (lo, hi) in enumerate(x_spans):
-            per_bank = BANK // (hi - lo)
-            sums.append([])
-            groups.append([range(u0, u0 + per_bank) for u0 in range(0, N_TILES, per_bank)])
-            for g, tiles in enumerate(groups[q]):
-                bank = psum.tile([P, per_bank, hi - lo], F32, name="sums", tag="bank_%d" % (J // SUB - 1 - lo // SUB - g))
-                first = True
+        def open_banks(lo, hi, first_bank, per_bank):
+            groups = []
+            for u0 in range(0, N_TILES, per_bank):
+                bank = psum.tile([P, per_bank, hi - lo], F32, name="sums", tag="bank_%d" % (first_bank + u0 // per_bank))
+                groups.append((bank, range(u0, u0 + per_bank)))
+            return groups
+
+        def tier_passes(groups, codes, plane, lo, hi, opens, closes):
+            for bank, tiles in groups:
                 for u in tiles:
-                    sums[q].append(bank[:, u - tiles[0], :])
-                    n0 = u * P
-                    for codes, plane in ((cq_codes, cq_plane), (cr_codes, cr_plane)):
-                        for s0 in range(lo, hi, SUB):
-                            nc.tensor.matmul_mx(
-                                out=bank[:, u - tiles[0], s0 - lo : s0 - lo + SUB],
-                                lhsT=wx_codes[:, 2 * n0 : 2 * (n0 + P)].bitcast(FP4X4), lhsT_scale=wx_plane[:, n0 : n0 + P],
-                                rhs=codes[:, s0 : s0 + SUB].bitcast(FP8X4), rhs_scale=plane[:, s0 : s0 + SUB], start=first, stop=False,
-                            )
-                            first = False
+                    for s0 in range(lo, hi, SUB):
+                        first = u == tiles[0] and s0 == lo
+                        final = u == tiles[-1] and s0 + SUB == hi
+                        wx_pass(bank[:, u - tiles[0], s0 - lo : s0 - lo + SUB], u, codes, plane, s0, s0 + SUB, opens and first, closes and final)
 
-        x_bf = [keep.tile([P, w * PACK], BF16, name="x_bf", tag="woven_x_%d" % q, align_bytes=64) for q, w in enumerate(X_WIDTHS)]
+        def x_passes(groups, lo, hi, closes):
+            for bank, tiles in groups:
+                for u in tiles:
+                    wt_pass(bank[:, u - tiles[0], :], u, lo, hi, False, closes and u == tiles[-1])
 
-        def gather(dst, t, lo, hi):
+        early_groups = []
+        for q, (lo, hi) in enumerate(x_spans[:3]):
+            groups = open_banks(lo, hi, 2 * q, 2)
+            for group in groups:
+                tier_passes([group], cr_codes, cr_plane, lo, hi, True, False)
+                tier_passes([group], cq_codes, cq_plane, lo, hi, False, False)
+            early_groups.append(groups)
+
+        x_bf = [keep.tile([P, HALF * PACK], BF16, name="x_bf_%d" % h, align_bytes=64) for h in range(2)]
+        picked = keep.tile([P, PACK, J], F32, name="picked", tag="rows_%d" % (EARLY_LOADS - 1), align_bytes=64)
+
+        def gather(t, lo, hi, dst=None):
+            dst = picked[:, t, lo:hi] if dst is None else dst
             nc.vector.tensor_tensor(dst, planes[t][:].indirect(offsets[:, lo // 16 : hi // 16]), wgt_sb[:, lo:hi], ALU.mult)
+
+        def x_part(lo, hi):
+            h = lo // HALF
+            return x_bf[h][:, (lo - h * HALF) * PACK : (hi - h * HALF) * PACK]
+
+        def weave_pair(t, lo, hi, copy):
+            copy(woven(x_part(lo, hi))[:, :, t : t + 2, :], planar(picked[:, t : t + 2, lo:hi]))
+
+        def quantise_x(lo, hi):
+            nc.vector.quantize_mx(out=xq_codes[:, lo:hi].bitcast(FP8X4), scales=xq_plane[:, lo:hi], in_=x_part(lo, hi))
 
         out_rows = out.rearrange("(u p) j -> p u j", p=P)
 
-        def finish(q):
+        for lo in (0, HALF):
+            gather(0, lo, lo + HALF)
+        for lo in (0, HALF):
+            gather(1, lo, lo + HALF)
+            weave_pair(0, lo, lo + HALF, nc.scalar.copy)
+        gather(2, 0, EARLY)
+
+        def store(groups, lo, hi):
+            sums = {u: bank[:, u - tiles[0], :] for bank, tiles in groups for u in tiles}
+            for u0 in (0, 2):
+                result = keep.tile([P, 2, hi - lo], F32, name="result_%d_%d" % (lo, u0))
+                for u in (u0, u0 + 1):
+                    nc.scalar.activation(result[:, u - u0, :], sums[u], ACT.Silu, bias=bias[:, u : u + 1])
+                queue = nc.scalar if hi == J and u0 == 2 else nc.sync
+                queue.dma_start(out_rows[:, u0 : u0 + 2, lo:hi], result[:])
+
+        def finish_early(q):
             lo, hi = x_spans[q]
-            nc.vector.quantize_mx(out=xq_codes[:, lo:hi].bitcast(FP8X4), scales=xq_plane[:, lo:hi], in_=x_bf[q][:])
-            for tiles in groups[q]:
-                for u in tiles:
-                    n0 = u * P
-                    nc.tensor.matmul_mx(
-                        out=sums[q][u],
-                        lhsT=wt_codes[:, 4 * n0 : 4 * (n0 + P)].bitcast(FP8X4), lhsT_scale=wt_plane[:, n0 : n0 + P],
-                        rhs=xq_codes[:, lo:hi].bitcast(FP8X4), rhs_scale=xq_plane[:, lo:hi], start=False, stop=(u == tiles[-1]),
-                    )
-            for g, tiles in enumerate((range(0, 2), range(2, 4))):
-                result = keep.tile([P, len(tiles), hi - lo], F32, name="result_%d_%d" % (q, g))
-                for u in tiles:
-                    nc.scalar.activation(result[:, u - tiles[0], :], sums[q][u], ACT.Silu, bias=bias[:, u : u + 1])
-                nc.sync.dma_start(out_rows[:, tiles[0] : tiles[-1] + 1, lo:hi], result[:])
+            quantise_x(lo, hi)
+            x_passes(early_groups[q], lo, hi, True)
+            store(early_groups[q], lo, hi)
 
-        early = keep.tile([P, PACK, EARLY], F32, name="early", tag="rows_%d" % (len(c_spans) - 1), align_bytes=64)
+        def finish_late(lo, hi, groups):
+            x_passes(groups, lo, hi, False)
+            tier_passes(groups, cr_codes, cr_plane, lo, hi, False, True)
+            store(groups, lo, hi)
 
-        def weave_pair(q, t, engine_copy):
-            lo, hi = x_spans[q]
-            engine_copy(woven(x_bf[q][:])[:, :, t : t + 2, :], planar(early[:, t : t + 2, lo:hi]))
-
-        def last_plane(q):
-            lo, hi = x_spans[q]
-            gather(early[:, PACK - 1, lo:hi], PACK - 1, lo, hi)
-
-        last = len(x_spans) - 1
-
-        late = keep.tile([P, PACK, J - EARLY], F32, name="late", align_bytes=64)
-
-        def late_plane(t):
-            gather(late[:, t, :], t, EARLY, J)
-
-        gather(early[:, 0, :EARLY], 0, 0, EARLY)
-        split = x_spans[1][1]
-        gather(early[:, 1, :split], 1, 0, split)
-        for q in range(2):
-            weave_pair(q, 0, nc.scalar.copy)
-        gather(early[:, 1, split:EARLY], 1, split, EARLY)
-        for q in range(2, last):
-            weave_pair(q, 0, nc.scalar.copy)
-        gather(early[:, 2, :EARLY], 2, 0, EARLY)
-
-        last_plane(0)
-        weave_pair(0, 2, nc.scalar.copy)
-        last_plane(1)
-        finish(0)
-        weave_pair(1, 2, nc.vector.tensor_copy)
-        last_plane(2)
-        finish(1)
-        weave_pair(2, 2, nc.vector.tensor_copy)
-        last_plane(3)
-        finish(2)
-        late_plane(0)
-        weave_pair(3, 2, nc.vector.tensor_copy)
-        late_plane(1)
-        finish(3)
-        late_plane(2)
-        late_plane(3)
-        nc.vector.tensor_copy(woven(x_bf[last][:]), planar(late[:]))
-        finish(last)
+        for q in range(3):
+            gather(3, *x_spans[q])
+            weave_pair(2, *x_spans[q], nc.scalar.copy)
+        finish_early(0)
+        weave_c(5)
+        first_tier(5)
+        finish_early(1)
+        late_picked = keep.tile([P, 2, J - EARLY], F32, name="late_picked", tag="late", align_bytes=64)
+        gather(2, EARLY, J, late_picked[:, 0, :])
+        finish_early(2)
+        late_groups = []
+        for g, lo in enumerate(range(EARLY, J, SUB)):
+            late_groups.append(open_banks(lo, lo + SUB, 2 * g, 2))
+            tier_passes(late_groups[g], cq_codes, cq_plane, lo, lo + SUB, True, False)
+        gather(3, EARLY, J, late_picked[:, 1, :])
+        for g, lo in enumerate(range(EARLY, J, SUB)):
+            late_rest = keep.tile([P, SUB * PACK], BF16, name="late_rest", tag="late_rest", align_bytes=64)
+            residual(lo, late_rest[:])
+            if g == 0:
+                nc.vector.tensor_copy(woven(x_part(EARLY, J))[:, :, 2:4, :], planar(late_picked[:]))
+            nc.vector.quantize_mx(out=cr_codes[:, lo : lo + SUB].bitcast(FP8X4), scales=cr_plane[:, lo : lo + SUB], in_=late_rest[:])
+            if g == 0:
+                quantise_x(EARLY, J)
+            finish_late(lo, lo + SUB, late_groups[g])

@@ -1,7 +1,6 @@
 from contextlib import ExitStack
 
 import concourse.mybir as mybir
-from concourse.masks import make_identity
 
 K, L, N, T, J = 512, 512, 512, 2048, 1024
 FLOPS = 2 * N * J * (K + 2 * L) + 2 * L * L * J
@@ -23,8 +22,8 @@ SUB = 128
 BANK = 512
 N_TILES = N // P
 HALF = J // 2
-C_WIDTHS = (128, 128, 256, 256, 256)
-EARLY_LOADS = 4
+C_WIDTHS = (256, 256, 256, 256)
+EARLY_LOADS = 3
 T_WIDTHS = (128, 128, 128, 128, 256, 256)
 EARLY_TIERS = 5
 EARLY = 768
@@ -63,10 +62,8 @@ def tile_list_silu_kernel(tc, xT, wgt, wt_words, wt_scales, c, wx_words, wx_scal
         w_planes = keep.tile([P, 2 * N], U8, name="w_planes", align_bytes=64)
         wx_plane, wt_plane = w_planes[:, :N], w_planes[:, N:]
         bias = keep.tile([P, N_TILES], F32, name="bias")
-        warm = keep.tile([P, 1], F32, name="warm")
-        warm_out = keep.tile([P, 1], F32, name="warm_out")
-        eye = keep.tile([P, P], BF16, name="eye")
-        eye_bf = keep.tile([P, PACK * (PACK * P + 1)], BF16, name="eye_bf", tag="woven_c", align_bytes=64)
+        distance = keep.tile([P, PACK * P], BF16, name="distance", align_bytes=64)
+        eye_bf = keep.tile([P, PACK * PACK * P], BF16, name="eye_bf", tag="woven_c", align_bytes=64)
         eye_codes = keep.tile([P, PACK * P], U32, name="eye_codes", align_bytes=64)
         eye_plane = keep.tile([P, PACK * P], U8, name="eye_plane", align_bytes=64)
         cq_codes = keep.tile([P, J], U32, name="cq_codes", align_bytes=64)
@@ -77,13 +74,13 @@ def tile_list_silu_kernel(tc, xT, wgt, wt_words, wt_scales, c, wx_words, wx_scal
         xq_plane = keep.tile([P, J], U8, name="xq_plane", align_bytes=64)
         rest_bf = keep.tile([P, EARLY * PACK], BF16, name="rest_bf", align_bytes=64)
 
-        make_identity(nc, eye[:])
-        nc.vector.memset(warm[:], 0.0)
-        nc.scalar.activation(warm_out[:], warm[:], ACT.Silu)
-        nc.vector.memset(eye_bf[:].bitcast(I32), 0)
+        nc.gpsimd.iota(distance[:], [[1, PACK * P]], base=0, channel_multiplier=-PACK, allow_small_or_imprecise_dtypes=True)
+        last_slice = (PACK - 1) * PACK * P
+        nc.scalar.activation(eye_bf[:, last_slice : last_slice + 2], distance[:, :2], ACT.Silu, scale=0.0)
         nc.vector.memset(w_planes[:].bitcast(I32), 0)
-        diagonal = eye_bf[:].rearrange("p (t r) -> p t r", t=PACK)[:, :, 0 : PACK * P : PACK]
-        nc.vector.tensor_copy(diagonal, eye[:].unsqueeze(1).to_broadcast([P, PACK, P]))
+        for t in range(PACK):
+            skip = 2 if t == PACK - 1 else 0
+            nc.vector.tensor_scalar(eye_bf[:, t * PACK * P + skip : (t + 1) * PACK * P], distance[:, skip:], float(t), None, ALU.is_equal)
         nc.vector.quantize_mx(out=eye_codes[:].bitcast(FP8X4), scales=eye_plane[:], in_=eye_bf[:, : PACK * PACK * P])
         c_bf = keep.tile([P, J * PACK], BF16, name="c_bf", tag="woven_c", align_bytes=64)
 
@@ -102,20 +99,19 @@ def tile_list_silu_kernel(tc, xT, wgt, wt_words, wt_scales, c, wx_words, wx_scal
         for q in range(EARLY_LOADS):
             load_c(q)
         nc.sync.dma_start(offsets[:], offs)
-        nc.sync.dma_start(wgt_sb[:, :HALF], wgt[:, :HALF])
+        nc.sync.dma_start(wgt_sb[:], wgt)
         nc.sync.dma_start(planes[0][:], x_rows[:, 0, :])
-        nc.sync.dma_start(wgt_sb[:, HALF:], wgt[:, HALF:])
-        nc.sync.dma_start(planes[1][:], x_rows[:, 1, :])
-        for quad in range(4):
-            load_scales(wx_plane, wx_scales, quad)
-        nc.sync.dma_start(planes[2][:], x_rows[:, 2, :])
         for quad in range(4):
             load_scales(wt_plane, wt_scales, quad)
+        nc.sync.dma_start(planes[1][:], x_rows[:, 1, :])
+        nc.sync.dma_start(planes[2][:], x_rows[:, 2, :])
+        for quad in range(4):
+            load_scales(wx_plane, wx_scales, quad)
         nc.sync.dma_start(wx_codes[:].bitcast(I32), wx_words[0].bitcast(I32))
         nc.sync.dma_start(planes[3][:], x_rows[:, 3, :])
-        nc.sync.dma_start(wt_codes[:].bitcast(I32), wt_words[0].rearrange("p n t -> p (n t)").bitcast(I32))
         for q in range(EARLY_LOADS, len(c_spans)):
             load_c(q)
+        nc.sync.dma_start(wt_codes[:].bitcast(I32), wt_words[0].rearrange("p n t -> p (n t)").bitcast(I32))
         with nc.allow_non_contiguous_dma(reason="one bias value for each partition and tile of output rows"):
             nc.sync.dma_start(bias[:], b.rearrange("(t p) -> p t", p=P))
 
@@ -235,12 +231,11 @@ def tile_list_silu_kernel(tc, xT, wgt, wt_words, wt_scales, c, wx_words, wx_scal
 
         out_rows = out.rearrange("(u p) j -> p u j", p=P)
 
-        for lo in (0, HALF):
-            gather(0, lo, lo + HALF)
+        gather(0, 0, J)
         for lo in (0, HALF):
             gather(1, lo, lo + HALF)
-            weave_pair(0, lo, lo + HALF, nc.scalar.copy)
-        gather(2, 0, EARLY)
+            weave_pair(0, lo, min(lo + HALF, EARLY), nc.scalar.copy)
+        gather(2, 0, J)
 
         def store(groups, lo, hi):
             sums = {u: bank[:, u - tiles[0], :] for bank, tiles in groups for u in tiles}
@@ -264,25 +259,24 @@ def tile_list_silu_kernel(tc, xT, wgt, wt_words, wt_scales, c, wx_words, wx_scal
 
         for q in range(3):
             gather(3, *x_spans[q])
-            weave_pair(2, *x_spans[q], nc.scalar.copy)
+            weave_pair(2, *x_spans[q], nc.scalar.copy if q else nc.vector.tensor_copy)
         finish_early(0)
         weave_c(5)
-        first_tier(5)
         finish_early(1)
-        late_picked = keep.tile([P, 2, J - EARLY], F32, name="late_picked", tag="late", align_bytes=64)
-        gather(2, EARLY, J, late_picked[:, 0, :])
+        first_tier(5)
         finish_early(2)
         late_groups = []
         for g, lo in enumerate(range(EARLY, J, SUB)):
             late_groups.append(open_banks(lo, lo + SUB, 2 * g, 2))
             tier_passes(late_groups[g], cq_codes, cq_plane, lo, lo + SUB, True, False)
-        gather(3, EARLY, J, late_picked[:, 1, :])
+        gather(3, EARLY, J)
         for g, lo in enumerate(range(EARLY, J, SUB)):
             late_rest = keep.tile([P, SUB * PACK], BF16, name="late_rest", tag="late_rest", align_bytes=64)
             residual(lo, late_rest[:])
             if g == 0:
-                nc.vector.tensor_copy(woven(x_part(EARLY, J))[:, :, 2:4, :], planar(late_picked[:]))
+                late_x_bf = keep.tile([P, (J - EARLY) * PACK], BF16, name="late_x_bf", tag="late", align_bytes=64)
+                nc.vector.tensor_copy(woven(late_x_bf[:]), planar(picked[:, :, EARLY:]))
             nc.vector.quantize_mx(out=cr_codes[:, lo : lo + SUB].bitcast(FP8X4), scales=cr_plane[:, lo : lo + SUB], in_=late_rest[:])
             if g == 0:
-                quantise_x(EARLY, J)
+                nc.vector.quantize_mx(out=xq_codes[:, EARLY:].bitcast(FP8X4), scales=xq_plane[:, EARLY:], in_=late_x_bf[:])
             finish_late(lo, lo + SUB, late_groups[g])

@@ -61,7 +61,6 @@ def tile_list_silu_kernel(tc, xT, wgt, wt_words, wt_scales, c, wx_words, wx_scal
         wx_codes = keep.tile([P, N * 2], U8, name="wx_codes", align_bytes=64)
         w_planes = keep.tile([P, 2 * N], U8, name="w_planes", align_bytes=64)
         wx_plane, wt_plane = w_planes[:, :N], w_planes[:, N:]
-        bias = keep.tile([P, N_TILES], F32, name="bias")
         distance = keep.tile([P, PACK * P], BF16, name="distance", align_bytes=64)
         eye_bf = keep.tile([P, PACK * PACK * P], BF16, name="eye_bf", tag="woven_c", align_bytes=64)
         eye_codes = keep.tile([P, PACK * P], U32, name="eye_codes", align_bytes=64)
@@ -112,8 +111,6 @@ def tile_list_silu_kernel(tc, xT, wgt, wt_words, wt_scales, c, wx_words, wx_scal
         for q in range(EARLY_LOADS, len(c_spans)):
             load_c(q)
         nc.sync.dma_start(wt_codes[:].bitcast(I32), wt_words[0].rearrange("p n t -> p (n t)").bitcast(I32))
-        with nc.allow_non_contiguous_dma(reason="one bias value for each partition and tile of output rows"):
-            nc.sync.dma_start(bias[:], b.rearrange("(t p) -> p t", p=P))
 
         def quantise(codes, plane, source, lo, hi):
             nc.vector.quantize_mx(out=codes[:, lo:hi].bitcast(FP8X4), scales=plane[:, lo:hi], in_=source[:, lo * PACK : hi * PACK])
@@ -184,6 +181,10 @@ def tile_list_silu_kernel(tc, xT, wgt, wt_words, wt_scales, c, wx_words, wx_scal
                 quantise(cr_codes, cr_plane, rest_bf, 0, HALF)
         quantise(cr_codes, cr_plane, rest_bf, HALF, EARLY)
 
+        bias = keep.tile([P, N_TILES], F32, name="bias", tag="rows_1", align_bytes=64)
+        with nc.allow_non_contiguous_dma(reason="one bias value for each partition and tile of output rows"):
+            nc.scalar.dma_start(bias[:], b.rearrange("(t p) -> p t", p=P))
+
         def open_banks(lo, hi, first_bank, per_bank):
             groups = []
             for u0 in range(0, N_TILES, per_bank):
@@ -234,8 +235,8 @@ def tile_list_silu_kernel(tc, xT, wgt, wt_words, wt_scales, c, wx_words, wx_scal
         gather(0, 0, J)
         for lo in (0, HALF):
             gather(1, lo, lo + HALF)
-            weave_pair(0, lo, min(lo + HALF, EARLY), nc.scalar.copy)
-        gather(2, 0, J)
+            weave_pair(0, lo, lo + HALF, nc.scalar.copy)
+        gather(2, 0, EARLY)
 
         def store(groups, lo, hi):
             sums = {u: bank[:, u - tiles[0], :] for bank, tiles in groups for u in tiles}
@@ -259,24 +260,28 @@ def tile_list_silu_kernel(tc, xT, wgt, wt_words, wt_scales, c, wx_words, wx_scal
 
         for q in range(3):
             gather(3, *x_spans[q])
-            weave_pair(2, *x_spans[q], nc.scalar.copy if q else nc.vector.tensor_copy)
+            weave_pair(2, *x_spans[q], nc.scalar.copy)
         finish_early(0)
         weave_c(5)
-        finish_early(1)
         first_tier(5)
+        finish_early(1)
+        late_picked = keep.tile([P, 2, J - EARLY], F32, name="late_picked", tag="late", align_bytes=64)
+        gather(2, EARLY, J, late_picked[:, 0, :])
         finish_early(2)
         late_groups = []
         for g, lo in enumerate(range(EARLY, J, SUB)):
             late_groups.append(open_banks(lo, lo + SUB, 2 * g, 2))
             tier_passes(late_groups[g], cq_codes, cq_plane, lo, lo + SUB, True, False)
-        gather(3, EARLY, J)
+        gather(3, EARLY, J, late_picked[:, 1, :])
         for g, lo in enumerate(range(EARLY, J, SUB)):
             late_rest = keep.tile([P, SUB * PACK], BF16, name="late_rest", tag="late_rest", align_bytes=64)
             residual(lo, late_rest[:])
             if g == 0:
-                late_x_bf = keep.tile([P, (J - EARLY) * PACK], BF16, name="late_x_bf", tag="late", align_bytes=64)
-                nc.vector.tensor_copy(woven(late_x_bf[:]), planar(picked[:, :, EARLY:]))
-            nc.vector.quantize_mx(out=cr_codes[:, lo : lo + SUB].bitcast(FP8X4), scales=cr_plane[:, lo : lo + SUB], in_=late_rest[:])
-            if g == 0:
-                nc.vector.quantize_mx(out=xq_codes[:, EARLY:].bitcast(FP8X4), scales=xq_plane[:, EARLY:], in_=late_x_bf[:])
+                nc.vector.tensor_copy(woven(x_part(EARLY, J))[:, :, 2:4, :], planar(late_picked[:]))
+            steps = [
+                (cr_codes, cr_plane, late_rest[:]),
+                (xq_codes, xq_plane, x_part(lo, lo + SUB)),
+            ]
+            for codes, plane, source in steps if g == 0 else reversed(steps):
+                nc.vector.quantize_mx(out=codes[:, lo : lo + SUB].bitcast(FP8X4), scales=plane[:, lo : lo + SUB], in_=source)
             finish_late(lo, lo + SUB, late_groups[g])

@@ -77,6 +77,10 @@ def tile_list_silu_kernel(tc, xT, wgt, wt_words, wt_scales, c, wx_words, wx_scal
         last_slice = (PACK - 1) * PACK * P
         nc.scalar.activation(eye_bf[:, last_slice : last_slice + 2], distance[:, :2], ACT.Silu, scale=0.0)
         nc.vector.memset(w_planes[:].bitcast(I32), 0)
+        bias_rows = keep.tile([P, P], F32, name="bias_rows", align_bytes=64)
+        nc.vector.memset(bias_rows[:], 0.0)
+        eye_f32 = keep.tile([P, P], F32, name="eye_f32", align_bytes=64)
+        nc.vector.tensor_scalar(eye_f32[:], distance[:, 0 : PACK * P : PACK], 0.0, None, ALU.is_equal)
         for t in range(PACK):
             skip = 2 if t == PACK - 1 else 0
             nc.vector.tensor_scalar(eye_bf[:, t * PACK * P + skip : (t + 1) * PACK * P], distance[:, skip:], float(t), None, ALU.is_equal)
@@ -100,6 +104,7 @@ def tile_list_silu_kernel(tc, xT, wgt, wt_words, wt_scales, c, wx_words, wx_scal
         nc.sync.dma_start(offsets[:], offs)
         nc.sync.dma_start(wgt_sb[:], wgt)
         nc.sync.dma_start(planes[0][:], x_rows[:, 0, :])
+        nc.sync.dma_start(bias_rows[:N_TILES, :], b.rearrange("(u p) -> u p", p=P))
         for quad in range(4):
             load_scales(wt_plane, wt_scales, quad)
         nc.sync.dma_start(planes[1][:], x_rows[:, 1, :])
@@ -181,9 +186,10 @@ def tile_list_silu_kernel(tc, xT, wgt, wt_words, wt_scales, c, wx_words, wx_scal
                 quantise(cr_codes, cr_plane, rest_bf, 0, HALF)
         quantise(cr_codes, cr_plane, rest_bf, HALF, EARLY)
 
-        bias = keep.tile([P, N_TILES], F32, name="bias", tag="rows_1", align_bytes=64)
-        with nc.allow_non_contiguous_dma(reason="one bias value for each partition and tile of output rows"):
-            nc.scalar.dma_start(bias[:], b.rearrange("(t p) -> p t", p=P))
+        turned = psum.tile([P, P], F32, name="turned", tag="bank_4")
+        nc.tensor.transpose(turned[:], bias_rows[:], eye_f32[:])
+        bias = keep.tile([P, N_TILES], F32, name="bias", align_bytes=64)
+        nc.scalar.copy(bias[:], turned[:, :N_TILES])
 
         def open_banks(lo, hi, first_bank, per_bank):
             groups = []

@@ -27,7 +27,7 @@ EARLY_LOADS = 3
 T_WIDTHS = (128, 128, 128, 128, 256, 256)
 EARLY_TIERS = 5
 EARLY = 768
-VECTOR_TIERS = (0, 2, 5)
+VECTOR_TIERS = (0, 2)
 X_WIDTHS = (256, 256, 256, 256)
 LATE_WIDTHS = (256, 128, 128)
 
@@ -71,7 +71,7 @@ def tile_list_silu_kernel(tc, xT, wgt, wt_words, wt_scales, c, wx_words, wx_scal
         cr_plane = keep.tile([P, J], U8, name="cr_plane", align_bytes=64)
         xq_codes = keep.tile([P, J], U32, name="xq_codes", align_bytes=64)
         xq_plane = keep.tile([P, J], U8, name="xq_plane", align_bytes=64)
-        rest_bf = keep.tile([P, EARLY * PACK], BF16, name="rest_bf", align_bytes=64)
+        rest_bf = keep.tile([P, HALF * PACK], BF16, name="rest_bf", align_bytes=64)
 
         nc.gpsimd.iota(distance[:], [[1, PACK * P]], base=0, channel_multiplier=-PACK, allow_small_or_imprecise_dtypes=True)
         last_slice = (PACK - 1) * PACK * P
@@ -79,15 +79,20 @@ def tile_list_silu_kernel(tc, xT, wgt, wt_words, wt_scales, c, wx_words, wx_scal
         nc.vector.memset(w_planes[:].bitcast(I32), 0)
         bias_rows = keep.tile([P, P], F32, name="bias_rows", align_bytes=64)
         nc.vector.memset(bias_rows[:], 0.0)
-        eye_f32 = keep.tile([P, P], F32, name="eye_f32", align_bytes=64)
-        nc.vector.tensor_scalar(eye_f32[:], distance[:, 0 : PACK * P : PACK], 0.0, None, ALU.is_equal)
         for t in range(PACK):
             skip = 2 if t == PACK - 1 else 0
             nc.vector.tensor_scalar(eye_bf[:, t * PACK * P + skip : (t + 1) * PACK * P], distance[:, skip:], float(t), None, ALU.is_equal)
+        eye_f32 = keep.tile([P, P], F32, name="eye_f32", align_bytes=64)
+        nc.scalar.copy(eye_f32[:], eye_bf[:, 0 : PACK * P : PACK])
         nc.vector.quantize_mx(out=eye_codes[:].bitcast(FP8X4), scales=eye_plane[:], in_=eye_bf[:, : PACK * PACK * P])
         c_bf = keep.tile([P, J * PACK], BF16, name="c_bf", tag="woven_c", align_bytes=64)
 
-        late_c_bf = keep.tile([P, (J - EARLY) * PACK], BF16, name="late_c_bf", tag="late", align_bytes=64)
+        lower = keep.tile([P, 256 + 2 * HALF], F32, name="lower", align_bytes=64)
+        upper = keep.tile([P, HALF * PACK], BF16, name="upper", align_bytes=64)
+        x_bf = [lower[:, 256:].bitcast(BF16), upper[:]]
+        late_c_bf = x_bf[0][:, : (J - EARLY) * PACK]
+        late_picked = lower[:, :512].rearrange("p (t c) -> p t c", t=2)
+        first_pair = keep.tile([P, 2 * 256], F32, name="first_pair", align_bytes=64)
 
         c_rows = c.rearrange("(p t) j -> p t j", t=PACK)
         x_rows = xT.rearrange("(p t) n -> p t n", t=PACK)
@@ -99,11 +104,12 @@ def tile_list_silu_kernel(tc, xT, wgt, wt_words, wt_scales, c, wx_words, wx_scal
             lo, hi = c_spans[q]
             nc.sync.dma_start(c_f32[q][:], c_rows[:, :, lo:hi])
 
-        for q in range(EARLY_LOADS):
+        for q in range(EARLY_LOADS - 1):
             load_c(q)
         nc.sync.dma_start(offsets[:], offs)
         nc.sync.dma_start(wgt_sb[:], wgt)
         nc.sync.dma_start(planes[0][:], x_rows[:, 0, :])
+        load_c(EARLY_LOADS - 1)
         nc.sync.dma_start(bias_rows[:N_TILES, :], b.rearrange("(u p) -> u p", p=P))
         for quad in range(4):
             load_scales(wt_plane, wt_scales, quad)
@@ -131,7 +137,7 @@ def tile_list_silu_kernel(tc, xT, wgt, wt_words, wt_scales, c, wx_words, wx_scal
             if q in (0, 2):
                 return c_bf[:, : (hi - lo) * PACK]
             if q == EARLY_TIERS:
-                return late_c_bf[:]
+                return late_c_bf
             return c_bf[:, lo * PACK : hi * PACK]
 
         def weave_c(q):
@@ -176,17 +182,16 @@ def tile_list_silu_kernel(tc, xT, wgt, wt_words, wt_scales, c, wx_words, wx_scal
         for q in range(2):
             weave_c(q)
             first_tier(q)
-        for q in range(EARLY_TIERS):
-            if q + 2 < EARLY_TIERS:
-                weave_c(q + 2)
-                first_tier(q + 2)
-            for s0 in range(t_spans[q][0], t_spans[q][1], SUB):
-                residual(s0)
-            if t_spans[q][0] == HALF:
-                quantise(cr_codes, cr_plane, rest_bf, 0, HALF)
-        quantise(cr_codes, cr_plane, rest_bf, HALF, EARLY)
+        weave_c(2)
+        weave_c(3)
+        residual(0)
+        first_tier(2)
+        first_tier(3)
+        for s in (1, 2, 3):
+            residual(s * SUB)
+        quantise(cr_codes, cr_plane, rest_bf, 0, 256)
 
-        turned = psum.tile([P, P], F32, name="turned", tag="bank_4")
+        turned = psum.tile([P, P], F32, name="turned", tag="bank_3")
         nc.tensor.transpose(turned[:], bias_rows[:], eye_f32[:])
         bias = keep.tile([P, N_TILES], F32, name="bias", align_bytes=64)
         nc.scalar.copy(bias[:], turned[:, :N_TILES])
@@ -211,16 +216,26 @@ def tile_list_silu_kernel(tc, xT, wgt, wt_words, wt_scales, c, wx_words, wx_scal
                 for u in tiles:
                     wt_pass(bank[:, u - tiles[0], :], u, lo, hi, False, closes and u == tiles[-1])
 
+        picked = keep.tile([P, PACK, J], F32, name="picked", tag="rows_1", align_bytes=64)
+        nc.vector.tensor_tensor(picked[:, 0, :], planes[0][:].indirect(offsets[:]), wgt_sb[:], ALU.mult)
+        weave_c(4)
+        first_tier(4)
+        quantise(cr_codes, cr_plane, rest_bf, 256, HALF)
+
         early_groups = []
-        for q, (lo, hi) in enumerate(x_spans[:3]):
+
+        def open_early(q):
+            lo, hi = x_spans[q]
             groups = open_banks(lo, hi, 2 * q, 2)
             for group in groups:
-                tier_passes([group], cr_codes, cr_plane, lo, hi, True, False)
-                tier_passes([group], cq_codes, cq_plane, lo, hi, False, False)
+                tier_passes([group], cq_codes, cq_plane, lo, hi, True, False)
+            for group in groups:
+                tier_passes([group], cr_codes, cr_plane, lo, hi, False, False)
             early_groups.append(groups)
 
-        x_bf = [keep.tile([P, HALF * PACK], BF16, name="x_bf_%d" % h, align_bytes=64) for h in range(2)]
-        picked = keep.tile([P, PACK, J], F32, name="picked", tag="rows_%d" % (EARLY_LOADS - 1), align_bytes=64)
+        open_early(0)
+        open_early(1)
+
 
         def gather(t, lo, hi, dst=None):
             dst = picked[:, t, lo:hi] if dst is None else dst
@@ -238,11 +253,13 @@ def tile_list_silu_kernel(tc, xT, wgt, wt_words, wt_scales, c, wx_words, wx_scal
 
         out_rows = out.rearrange("(u p) j -> p u j", p=P)
 
-        gather(0, 0, J)
         for lo in (0, HALF):
             gather(1, lo, lo + HALF)
             weave_pair(0, lo, lo + HALF, nc.scalar.copy)
-        gather(2, 0, EARLY)
+        first_planes = first_pair[:].rearrange("p (t c) -> p t c", t=2)
+        gather(2, *x_spans[0], first_planes[:, 0, :])
+        gather(2, x_spans[0][1], EARLY)
+        gather(2, EARLY, J, late_picked[:, 0, :])
 
         def store(groups, lo, hi):
             sums = {u: bank[:, u - tiles[0], :] for bank, tiles in groups for u in tiles}
@@ -250,8 +267,13 @@ def tile_list_silu_kernel(tc, xT, wgt, wt_words, wt_scales, c, wx_words, wx_scal
                 result = keep.tile([P, 2, hi - lo], F32, name="result_%d_%d" % (lo, u0))
                 for u in (u0, u0 + 1):
                     nc.scalar.activation(result[:, u - u0, :], sums[u], ACT.Silu, bias=bias[:, u : u + 1])
-                queue = nc.scalar if hi == J and u0 == 2 else nc.sync
+                queue = nc.scalar if lo >= EARLY and u0 == 2 else nc.sync
                 queue.dma_start(out_rows[:, u0 : u0 + 2, lo:hi], result[:])
+
+        def finish_late(lo, hi, groups):
+            x_passes(groups, lo, hi, False)
+            tier_passes(groups, cr_codes, cr_plane, lo, hi, False, True)
+            store(groups, lo, hi)
 
         def finish_early(q):
             lo, hi = x_spans[q]
@@ -259,20 +281,22 @@ def tile_list_silu_kernel(tc, xT, wgt, wt_words, wt_scales, c, wx_words, wx_scal
             x_passes(early_groups[q], lo, hi, True)
             store(early_groups[q], lo, hi)
 
-        def finish_late(lo, hi, groups):
-            x_passes(groups, lo, hi, False)
-            tier_passes(groups, cr_codes, cr_plane, lo, hi, False, True)
-            store(groups, lo, hi)
-
-        for q in range(3):
+        gather(3, *x_spans[0], first_planes[:, 1, :])
+        nc.scalar.copy(woven(x_part(*x_spans[0]))[:, :, 2:4, :], planar(first_planes))
+        for q in (1, 2):
             gather(3, *x_spans[q])
             weave_pair(2, *x_spans[q], nc.scalar.copy)
         finish_early(0)
-        weave_c(5)
-        first_tier(5)
+        nc.gpsimd.tensor_scalar(
+            late_c_bf.rearrange("p (c t) -> p c t", t=PACK), c_columns(EARLY, J).rearrange("p t c -> p c t"), 1.0, 0.0, ALU.mult, ALU.add,
+        )
+        held_rest = first_pair[:].bitcast(BF16)
+        for g, lo in enumerate(range(HALF, EARLY, SUB)):
+            residual(lo, held_rest[:, g * SUB * PACK : (g + 1) * SUB * PACK])
         finish_early(1)
-        late_picked = keep.tile([P, 2, J - EARLY], F32, name="late_picked", tag="late", align_bytes=64)
-        gather(2, EARLY, J, late_picked[:, 0, :])
+        nc.vector.quantize_mx(out=cr_codes[:, HALF:EARLY].bitcast(FP8X4), scales=cr_plane[:, HALF:EARLY], in_=held_rest)
+        first_tier(EARLY_TIERS)
+        open_early(2)
         finish_early(2)
         late_groups = []
         for g, lo in enumerate(range(EARLY, J, SUB)):
@@ -283,7 +307,7 @@ def tile_list_silu_kernel(tc, xT, wgt, wt_words, wt_scales, c, wx_words, wx_scal
             late_rest = keep.tile([P, SUB * PACK], BF16, name="late_rest", tag="late_rest", align_bytes=64)
             residual(lo, late_rest[:])
             if g == 0:
-                nc.vector.tensor_copy(woven(x_part(EARLY, J))[:, :, 2:4, :], planar(late_picked[:]))
+                nc.vector.tensor_copy(woven(x_part(EARLY, J))[:, :, 2:4, :], planar(late_picked))
             steps = [
                 (cr_codes, cr_plane, late_rest[:]),
                 (xq_codes, xq_plane, x_part(lo, lo + SUB)),

@@ -29,7 +29,7 @@ EARLY_TIERS = 5
 EARLY = 768
 VECTOR_TIERS = (0, 2)
 X_WIDTHS = (256, 256, 256, 256)
-LATE_WIDTHS = (256, 128, 128)
+CHUNK = 256
 
 
 def spans(widths):
@@ -87,12 +87,20 @@ def tile_list_silu_kernel(tc, xT, wgt, wt_words, wt_scales, c, wx_words, wx_scal
         nc.vector.quantize_mx(out=eye_codes[:].bitcast(FP8X4), scales=eye_plane[:], in_=eye_bf[:, : PACK * PACK * P])
         c_bf = keep.tile([P, J * PACK], BF16, name="c_bf", tag="woven_c", align_bytes=64)
 
-        lower = keep.tile([P, 256 + 2 * HALF], F32, name="lower", align_bytes=64)
-        upper = keep.tile([P, HALF * PACK], BF16, name="upper", align_bytes=64)
-        x_bf = [lower[:, 256:].bitcast(BF16), upper[:]]
-        late_c_bf = x_bf[0][:, : (J - EARLY) * PACK]
-        late_picked = lower[:, :512].rearrange("p (t c) -> p t c", t=2)
-        first_pair = keep.tile([P, 2 * 256], F32, name="first_pair", align_bytes=64)
+        x_first = keep.tile([P, CHUNK * PACK], BF16, name="x_first", align_bytes=64)
+        x_upper = keep.tile([P, HALF * PACK], BF16, name="x_upper", align_bytes=64)
+        second_pair = keep.tile([P, 2 * CHUNK], F32, name="second_pair", align_bytes=64)
+        shared = keep.tile([P, 12 * CHUNK], F32, name="shared", align_bytes=64)
+
+        def two_rows(first, second):
+            step = second - first
+            return shared[:, first * CHUNK : (first + 2 * step) * CHUNK].rearrange("p (t c) -> p t c", t=2)[:, :, :CHUNK]
+
+        late_c_bf = keep.tile([P, CHUNK * PACK], BF16, name="late_c_bf", align_bytes=64)[:]
+        held_rest = shared[:, : 2 * CHUNK].bitcast(BF16)
+        x_parts = [x_first[:], shared[:, 4 * CHUNK : 6 * CHUNK].bitcast(BF16), x_upper[:, : CHUNK * PACK], x_upper[:, CHUNK * PACK :]]
+        last_pairs = [two_rows(0, 6), second_pair[:].rearrange("p (t c) -> p t c", t=2), two_rows(2, 7), two_rows(3, 7)]
+        late_rest = x_parts[2]
 
         c_rows = c.rearrange("(p t) j -> p t j", t=PACK)
         x_rows = xT.rearrange("(p t) n -> p t n", t=PACK)
@@ -149,7 +157,7 @@ def tile_list_silu_kernel(tc, xT, wgt, wt_words, wt_scales, c, wx_words, wx_scal
             lo, hi = t_spans[q]
             nc.vector.quantize_mx(out=cq_codes[:, lo:hi].bitcast(FP8X4), scales=cq_plane[:, lo:hi], in_=tier_part(q))
             for s0 in range(lo, hi, SUB):
-                bank = psum.tile([P, PACK, SUB], F32, name="back", tag="bank_%d" % (s0 // SUB))
+                bank = psum.tile([P, PACK, SUB], F32, name="back", tag="bank_%d" % (s0 % EARLY // SUB))
                 for t in range(PACK):
                     nc.tensor.matmul_mx(
                         out=bank[:, t, :],
@@ -206,18 +214,15 @@ def tile_list_silu_kernel(tc, xT, wgt, wt_words, wt_scales, c, wx_words, wx_scal
         def tier_passes(groups, codes, plane, lo, hi, opens, closes):
             for bank, tiles in groups:
                 for u in tiles:
-                    for s0 in range(lo, hi, SUB):
-                        first = u == tiles[0] and s0 == lo
-                        final = u == tiles[-1] and s0 + SUB == hi
-                        wx_pass(bank[:, u - tiles[0], s0 - lo : s0 - lo + SUB], u, codes, plane, s0, s0 + SUB, opens and first, closes and final)
+                    wx_pass(bank[:, u - tiles[0], :], u, codes, plane, lo, hi, opens and u == tiles[0], closes and u == tiles[-1])
 
         def x_passes(groups, lo, hi, closes):
             for bank, tiles in groups:
                 for u in tiles:
                     wt_pass(bank[:, u - tiles[0], :], u, lo, hi, False, closes and u == tiles[-1])
 
-        picked = keep.tile([P, PACK, J], F32, name="picked", tag="rows_1", align_bytes=64)
-        nc.vector.tensor_tensor(picked[:, 0, :], planes[0][:].indirect(offsets[:]), wgt_sb[:], ALU.mult)
+        picked = keep.tile([P, 2 * J], F32, name="picked", tag="rows_1", align_bytes=64)
+        nc.vector.tensor_tensor(picked[:, :J], planes[0][:].indirect(offsets[:]), wgt_sb[:], ALU.mult)
         weave_c(4)
         first_tier(4)
         quantise(cr_codes, cr_plane, rest_bf, 256, HALF)
@@ -235,83 +240,76 @@ def tile_list_silu_kernel(tc, xT, wgt, wt_words, wt_scales, c, wx_words, wx_scal
 
         open_early(0)
         open_early(1)
-
+        early_groups.append(open_banks(*x_spans[2], 6, 2))
+        tier_passes(early_groups[2], cq_codes, cq_plane, *x_spans[2], True, False)
 
         def gather(t, lo, hi, dst=None):
-            dst = picked[:, t, lo:hi] if dst is None else dst
+            dst = picked[:, t * J + lo : t * J + hi] if dst is None else dst
             nc.vector.tensor_tensor(dst, planes[t][:].indirect(offsets[:, lo // 16 : hi // 16]), wgt_sb[:, lo:hi], ALU.mult)
 
-        def x_part(lo, hi):
-            h = lo // HALF
-            return x_bf[h][:, (lo - h * HALF) * PACK : (hi - h * HALF) * PACK]
+        def pair_rows(t, lo, hi):
+            return picked[:, t * J : (t + 2) * J].rearrange("p (t c) -> p t c", t=2)[:, :, lo:hi]
 
-        def weave_pair(t, lo, hi, copy):
-            copy(woven(x_part(lo, hi))[:, :, t : t + 2, :], planar(picked[:, t : t + 2, lo:hi]))
+        def quantise_x(q):
+            lo, hi = x_spans[q]
+            nc.vector.quantize_mx(out=xq_codes[:, lo:hi].bitcast(FP8X4), scales=xq_plane[:, lo:hi], in_=x_parts[q])
 
-        def quantise_x(lo, hi):
-            nc.vector.quantize_mx(out=xq_codes[:, lo:hi].bitcast(FP8X4), scales=xq_plane[:, lo:hi], in_=x_part(lo, hi))
+        def gpsimd_round(dst, source):
+            nc.gpsimd.tensor_scalar(dst, source, 1.0, 0.0, ALU.mult, ALU.add)
 
         out_rows = out.rearrange("(u p) j -> p u j", p=P)
 
-        for lo in (0, HALF):
-            gather(1, lo, lo + HALF)
-            weave_pair(0, lo, lo + HALF, nc.scalar.copy)
-        first_planes = first_pair[:].rearrange("p (t c) -> p t c", t=2)
-        gather(2, *x_spans[0], first_planes[:, 0, :])
-        gather(2, x_spans[0][1], EARLY)
-        gather(2, EARLY, J, late_picked[:, 0, :])
+        gather(1, 0, HALF)
+        for q in (0, 1):
+            nc.scalar.copy(woven(x_parts[q])[:, :, 0:2, :], planar(pair_rows(0, *x_spans[q])))
+        gather(1, HALF, J)
+        nc.scalar.copy(woven(x_upper[:])[:, :, 0:2, :], planar(pair_rows(0, HALF, J)))
+        gather(2, *x_spans[0], last_pairs[0][:, 0, :])
+        gather(2, *x_spans[1], last_pairs[1][:, 0, :])
+        gather(2, HALF, J, shared[:, 2 * CHUNK : 4 * CHUNK])
 
         def store(groups, lo, hi):
-            sums = {u: bank[:, u - tiles[0], :] for bank, tiles in groups for u in tiles}
-            for u0 in (0, 2):
-                result = keep.tile([P, 2, hi - lo], F32, name="result_%d_%d" % (lo, u0))
-                for u in (u0, u0 + 1):
-                    nc.scalar.activation(result[:, u - u0, :], sums[u], ACT.Silu, bias=bias[:, u : u + 1])
-                queue = nc.scalar if lo >= EARLY and u0 == 2 else nc.sync
-                queue.dma_start(out_rows[:, u0 : u0 + 2, lo:hi], result[:])
-
-        def finish_late(lo, hi, groups):
-            x_passes(groups, lo, hi, False)
-            tier_passes(groups, cr_codes, cr_plane, lo, hi, False, True)
-            store(groups, lo, hi)
+            for bank, tiles in groups:
+                result = keep.tile([P, len(tiles), hi - lo], F32, name="result_%d_%d" % (lo, tiles[0]))
+                for u in tiles:
+                    nc.scalar.activation(result[:, u - tiles[0], :], bank[:, u - tiles[0], :], ACT.Silu, bias=bias[:, u : u + 1])
+                nc.sync.dma_start(out_rows[:, tiles[0] : tiles[-1] + 1, lo:hi], result[:])
 
         def finish_early(q):
             lo, hi = x_spans[q]
-            quantise_x(lo, hi)
+            quantise_x(q)
             x_passes(early_groups[q], lo, hi, True)
             store(early_groups[q], lo, hi)
 
-        gather(3, *x_spans[0], first_planes[:, 1, :])
-        nc.scalar.copy(woven(x_part(*x_spans[0]))[:, :, 2:4, :], planar(first_planes))
+        def gpsimd_pair(q):
+            gpsimd_round(x_parts[q].rearrange("p (c t) -> p c t", t=PACK)[:, :, 2:4], last_pairs[q].rearrange("p t c -> p c t"))
+
+        gather(3, *x_spans[0], last_pairs[0][:, 1, :])
+        nc.scalar.copy(woven(x_parts[0])[:, :, 2:4, :], planar(last_pairs[0]))
+        weave_c(EARLY_TIERS)
         for q in (1, 2):
-            gather(3, *x_spans[q])
-            weave_pair(2, *x_spans[q], nc.scalar.copy)
+            gather(3, *x_spans[q], last_pairs[q][:, 1, :])
         finish_early(0)
-        nc.gpsimd.tensor_scalar(
-            late_c_bf.rearrange("p (c t) -> p c t", t=PACK), c_columns(EARLY, J).rearrange("p t c -> p c t"), 1.0, 0.0, ALU.mult, ALU.add,
-        )
-        held_rest = first_pair[:].bitcast(BF16)
+        nc.vector.tensor_copy(woven(x_parts[1])[:, :, 2:4, :], planar(last_pairs[1]))
+        gpsimd_pair(2)
         for g, lo in enumerate(range(HALF, EARLY, SUB)):
             residual(lo, held_rest[:, g * SUB * PACK : (g + 1) * SUB * PACK])
         finish_early(1)
-        nc.vector.quantize_mx(out=cr_codes[:, HALF:EARLY].bitcast(FP8X4), scales=cr_plane[:, HALF:EARLY], in_=held_rest)
         first_tier(EARLY_TIERS)
-        open_early(2)
+        nc.vector.quantize_mx(out=cr_codes[:, HALF:EARLY].bitcast(FP8X4), scales=cr_plane[:, HALF:EARLY], in_=held_rest)
+        tier_passes(early_groups[2], cr_codes, cr_plane, *x_spans[2], False, False)
         finish_early(2)
-        late_groups = []
+        gather(3, *x_spans[3], last_pairs[3][:, 1, :])
+        gpsimd_pair(3)
         for g, lo in enumerate(range(EARLY, J, SUB)):
-            late_groups.append(open_banks(lo, lo + SUB, 2 * g, 2))
-            tier_passes(late_groups[g], cq_codes, cq_plane, lo, lo + SUB, True, False)
-        gather(3, EARLY, J, late_picked[:, 1, :])
-        for g, lo in enumerate(range(EARLY, J, SUB)):
-            late_rest = keep.tile([P, SUB * PACK], BF16, name="late_rest", tag="late_rest", align_bytes=64)
-            residual(lo, late_rest[:])
-            if g == 0:
-                nc.vector.tensor_copy(woven(x_part(EARLY, J))[:, :, 2:4, :], planar(late_picked))
-            steps = [
-                (cr_codes, cr_plane, late_rest[:]),
-                (xq_codes, xq_plane, x_part(lo, lo + SUB)),
-            ]
-            for codes, plane, source in steps if g == 0 else reversed(steps):
-                nc.vector.quantize_mx(out=codes[:, lo : lo + SUB].bitcast(FP8X4), scales=plane[:, lo : lo + SUB], in_=source)
-            finish_late(lo, lo + SUB, late_groups[g])
+            residual(lo, late_rest[:, g * SUB * PACK : (g + 1) * SUB * PACK])
+        late_groups = [
+            (psum.tile([P, 1, CHUNK], F32, name="sums", tag="bank_%d" % bank), range(u, u + 1)) for u, bank in enumerate((2, 3, 0, 1))
+        ]
+        tier_passes(late_groups, cq_codes, cq_plane, EARLY, J, True, False)
+        nc.vector.quantize_mx(out=cr_codes[:, EARLY:].bitcast(FP8X4), scales=cr_plane[:, EARLY:], in_=late_rest)
+        quantise_x(3)
+        for group in late_groups:
+            tier_passes([group], cr_codes, cr_plane, EARLY, J, False, False)
+            x_passes([group], EARLY, J, True)
+            store([group], EARLY, J)

@@ -87,20 +87,24 @@ def tile_list_silu_kernel(tc, xT, wgt, wt_words, wt_scales, c, wx_words, wx_scal
         nc.vector.quantize_mx(out=eye_codes[:].bitcast(FP8X4), scales=eye_plane[:], in_=eye_bf[:, : PACK * PACK * P])
         c_bf = keep.tile([P, J * PACK], BF16, name="c_bf", tag="woven_c", align_bytes=64)
 
-        x_first = keep.tile([P, CHUNK * PACK], BF16, name="x_first", align_bytes=64)
+        x_lower = keep.tile([P, HALF * PACK], BF16, name="x_lower", align_bytes=64)
         x_upper = keep.tile([P, HALF * PACK], BF16, name="x_upper", align_bytes=64)
         second_pair = keep.tile([P, 2 * CHUNK], F32, name="second_pair", align_bytes=64)
-        shared = keep.tile([P, 12 * CHUNK], F32, name="shared", align_bytes=64)
+        shared = keep.tile([P, 22 * SUB], U32, name="shared", align_bytes=64)
+
+        def region(first, last, dtype):
+            return shared[:, first * SUB : last * SUB].bitcast(dtype)
 
         def two_rows(first, second):
-            step = second - first
-            return shared[:, first * CHUNK : (first + 2 * step) * CHUNK].rearrange("p (t c) -> p t c", t=2)[:, :, :CHUNK]
+            return region(first, 2 * second - first, F32).rearrange("p (t c) -> p t c", t=2)[:, :, :CHUNK]
 
-        late_c_bf = keep.tile([P, CHUNK * PACK], BF16, name="late_c_bf", align_bytes=64)[:]
-        held_rest = shared[:, : 2 * CHUNK].bitcast(BF16)
-        x_parts = [x_first[:], shared[:, 4 * CHUNK : 6 * CHUNK].bitcast(BF16), x_upper[:, : CHUNK * PACK], x_upper[:, CHUNK * PACK :]]
-        last_pairs = [two_rows(0, 6), second_pair[:].rearrange("p (t c) -> p t c", t=2), two_rows(2, 7), two_rows(3, 7)]
-        late_rest = x_parts[2]
+        late_c_bf = region(14, 18, BF16)
+        late_rest = region(0, 4, BF16)
+        last_plane = region(11, 15, F32)
+        held_rest = second_pair[:].bitcast(BF16)
+        x_parts = [half[:, h * CHUNK * PACK : (h + 1) * CHUNK * PACK] for half in (x_lower, x_upper) for h in (0, 1)]
+        x_words = [xq_codes[:, lo:hi] for lo, hi in x_spans]
+        last_pairs = [two_rows(8, 10), second_pair[:].rearrange("p (t c) -> p t c", t=2), two_rows(0, 11), two_rows(4, 13)]
 
         c_rows = c.rearrange("(p t) j -> p t j", t=PACK)
         x_rows = xT.rearrange("(p t) n -> p t n", t=PACK)
@@ -184,7 +188,7 @@ def tile_list_silu_kernel(tc, xT, wgt, wt_words, wt_scales, c, wx_words, wx_scal
             n0 = u * P
             nc.tensor.matmul_mx(
                 out=dst, lhsT=wt_codes[:, 4 * n0 : 4 * (n0 + P)].bitcast(FP8X4), lhsT_scale=wt_plane[:, n0 : n0 + P],
-                rhs=xq_codes[:, lo:hi].bitcast(FP8X4), rhs_scale=xq_plane[:, lo:hi], start=start, stop=stop,
+                rhs=x_words[lo // CHUNK].bitcast(FP8X4), rhs_scale=xq_plane[:, lo:hi], start=start, stop=stop,
             )
 
         for q in range(2):
@@ -252,7 +256,7 @@ def tile_list_silu_kernel(tc, xT, wgt, wt_words, wt_scales, c, wx_words, wx_scal
 
         def quantise_x(q):
             lo, hi = x_spans[q]
-            nc.vector.quantize_mx(out=xq_codes[:, lo:hi].bitcast(FP8X4), scales=xq_plane[:, lo:hi], in_=x_parts[q])
+            nc.vector.quantize_mx(out=x_words[q].bitcast(FP8X4), scales=xq_plane[:, lo:hi], in_=x_parts[q])
 
         def gpsimd_round(dst, source):
             nc.gpsimd.tensor_scalar(dst, source, 1.0, 0.0, ALU.mult, ALU.add)
@@ -260,13 +264,11 @@ def tile_list_silu_kernel(tc, xT, wgt, wt_words, wt_scales, c, wx_words, wx_scal
         out_rows = out.rearrange("(u p) j -> p u j", p=P)
 
         gather(1, 0, HALF)
-        for q in (0, 1):
-            nc.scalar.copy(woven(x_parts[q])[:, :, 0:2, :], planar(pair_rows(0, *x_spans[q])))
+        nc.scalar.copy(woven(x_lower[:])[:, :, 0:2, :], planar(pair_rows(0, 0, HALF)))
         gather(1, HALF, J)
         nc.scalar.copy(woven(x_upper[:])[:, :, 0:2, :], planar(pair_rows(0, HALF, J)))
-        gather(2, *x_spans[0], last_pairs[0][:, 0, :])
-        gather(2, *x_spans[1], last_pairs[1][:, 0, :])
-        gather(2, HALF, J, shared[:, 2 * CHUNK : 4 * CHUNK])
+        for q, span in enumerate(x_spans):
+            gather(2, *span, last_pairs[q][:, 0, :])
 
         def store(groups, lo, hi):
             for bank, tiles in groups:
@@ -284,13 +286,16 @@ def tile_list_silu_kernel(tc, xT, wgt, wt_words, wt_scales, c, wx_words, wx_scal
         def gpsimd_pair(q):
             gpsimd_round(x_parts[q].rearrange("p (c t) -> p c t", t=PACK)[:, :, 2:4], last_pairs[q].rearrange("p t c -> p c t"))
 
-        gather(3, *x_spans[0], last_pairs[0][:, 1, :])
-        nc.scalar.copy(woven(x_parts[0])[:, :, 2:4, :], planar(last_pairs[0]))
-        weave_c(EARLY_TIERS)
-        for q in (1, 2):
+        def gather_upper(lo, hi):
+            gather(3, lo, hi, last_plane[:, lo - HALF : hi - HALF])
+
+        for q in (0, 1):
             gather(3, *x_spans[q], last_pairs[q][:, 1, :])
+            nc.scalar.copy(woven(x_parts[q])[:, :, 2:4, :], planar(last_pairs[q]))
+        weave_c(EARLY_TIERS)
+        gather_upper(HALF + SUB, J - SUB)
         finish_early(0)
-        nc.vector.tensor_copy(woven(x_parts[1])[:, :, 2:4, :], planar(last_pairs[1]))
+        gather_upper(HALF, HALF + SUB)
         gpsimd_pair(2)
         for g, lo in enumerate(range(HALF, EARLY, SUB)):
             residual(lo, held_rest[:, g * SUB * PACK : (g + 1) * SUB * PACK])
@@ -298,8 +303,8 @@ def tile_list_silu_kernel(tc, xT, wgt, wt_words, wt_scales, c, wx_words, wx_scal
         first_tier(EARLY_TIERS)
         nc.vector.quantize_mx(out=cr_codes[:, HALF:EARLY].bitcast(FP8X4), scales=cr_plane[:, HALF:EARLY], in_=held_rest)
         tier_passes(early_groups[2], cr_codes, cr_plane, *x_spans[2], False, False)
+        gather_upper(J - SUB, J)
         finish_early(2)
-        gather(3, *x_spans[3], last_pairs[3][:, 1, :])
         gpsimd_pair(3)
         for g, lo in enumerate(range(EARLY, J, SUB)):
             residual(lo, late_rest[:, g * SUB * PACK : (g + 1) * SUB * PACK])

@@ -88,7 +88,7 @@ def tile_list_silu_kernel(tc, xT, wgt, wt_words, wt_scales, c, wx_words, wx_scal
         c_bf = keep.tile([P, J * PACK], BF16, name="c_bf", tag="woven_c", align_bytes=64)
 
         x_lower = keep.tile([P, HALF * PACK], BF16, name="x_lower", align_bytes=64)
-        x_upper = keep.tile([P, HALF * PACK], BF16, name="x_upper", align_bytes=64)
+        x_upper = keep.tile([P, (HALF + CHUNK) * PACK], BF16, name="x_upper", align_bytes=64)
         second_pair = keep.tile([P, 2 * CHUNK], F32, name="second_pair", align_bytes=64)
         shared = keep.tile([P, 22 * SUB], U32, name="shared", align_bytes=64)
 
@@ -99,10 +99,11 @@ def tile_list_silu_kernel(tc, xT, wgt, wt_words, wt_scales, c, wx_words, wx_scal
             return region(first, 2 * second - first, F32).rearrange("p (t c) -> p t c", t=2)[:, :, :CHUNK]
 
         late_c_bf = region(14, 18, BF16)
-        late_rest = region(0, 4, BF16)
+        late_rest = x_upper[:, SUB * PACK : (SUB + CHUNK) * PACK]
+        third_halves = x_upper[:].rearrange("p (h c t) -> p h c t", h=2, t=PACK)[:, :, :SUB, :]
         last_plane = region(11, 15, F32)
         held_rest = second_pair[:].bitcast(BF16)
-        x_parts = [half[:, h * CHUNK * PACK : (h + 1) * CHUNK * PACK] for half in (x_lower, x_upper) for h in (0, 1)]
+        x_parts = [x_lower[:, : CHUNK * PACK], x_lower[:, CHUNK * PACK :], None, x_upper[:, HALF * PACK :]]
         x_words = [xq_codes[:, lo:hi] for lo, hi in x_spans]
         last_pairs = [two_rows(8, 10), second_pair[:].rearrange("p (t c) -> p t c", t=2), two_rows(0, 11), two_rows(4, 13)]
 
@@ -266,7 +267,8 @@ def tile_list_silu_kernel(tc, xT, wgt, wt_words, wt_scales, c, wx_words, wx_scal
         gather(1, 0, HALF)
         nc.scalar.copy(woven(x_lower[:])[:, :, 0:2, :], planar(pair_rows(0, 0, HALF)))
         gather(1, HALF, J)
-        nc.scalar.copy(woven(x_upper[:])[:, :, 0:2, :], planar(pair_rows(0, HALF, J)))
+        nc.scalar.copy(woven(x_upper[:, : SUB * PACK])[:, :, 0:2, :], planar(pair_rows(0, HALF, HALF + SUB)))
+        nc.scalar.copy(woven(x_upper[:, (SUB + CHUNK) * PACK :])[:, :, 0:2, :], planar(pair_rows(0, HALF + SUB, J)))
         for q, span in enumerate(x_spans):
             gather(2, *span, last_pairs[q][:, 0, :])
 
@@ -296,7 +298,7 @@ def tile_list_silu_kernel(tc, xT, wgt, wt_words, wt_scales, c, wx_words, wx_scal
         gather_upper(HALF + SUB, J - SUB)
         finish_early(0)
         gather_upper(HALF, HALF + SUB)
-        gpsimd_pair(2)
+        gpsimd_round(third_halves[:, :, :, 2:4], last_pairs[2].rearrange("p t (h c) -> p h c t", h=2))
         for g, lo in enumerate(range(HALF, EARLY, SUB)):
             residual(lo, held_rest[:, g * SUB * PACK : (g + 1) * SUB * PACK])
         finish_early(1)
@@ -304,7 +306,13 @@ def tile_list_silu_kernel(tc, xT, wgt, wt_words, wt_scales, c, wx_words, wx_scal
         nc.vector.quantize_mx(out=cr_codes[:, HALF:EARLY].bitcast(FP8X4), scales=cr_plane[:, HALF:EARLY], in_=held_rest)
         tier_passes(early_groups[2], cr_codes, cr_plane, *x_spans[2], False, False)
         gather_upper(J - SUB, J)
-        finish_early(2)
+        for h, lo in enumerate(range(HALF, EARLY, SUB)):
+            nc.vector.quantize_mx(
+                out=xq_codes[:, lo : lo + SUB].bitcast(FP8X4), scales=xq_plane[:, lo : lo + SUB],
+                in_=third_halves[:, h, :, :].rearrange("p c t -> p (c t)"),
+            )
+        x_passes(early_groups[2], HALF, EARLY, True)
+        store(early_groups[2], HALF, EARLY)
         gpsimd_pair(3)
         for g, lo in enumerate(range(EARLY, J, SUB)):
             residual(lo, late_rest[:, g * SUB * PACK : (g + 1) * SUB * PACK])

@@ -275,9 +275,13 @@ def tile_list_silu_kernel(tc, xT, wgt, wt_words, wt_scales, c, wx_words, wx_scal
         def store(groups, lo, hi):
             for bank, tiles in groups:
                 result = keep.tile([P, len(tiles), hi - lo], F32, name="result_%d_%d" % (lo, tiles[0]))
+                one_by_one = lo == 0 and tiles[0] == 0
                 for u in tiles:
                     nc.scalar.activation(result[:, u - tiles[0], :], bank[:, u - tiles[0], :], ACT.Silu, bias=bias[:, u : u + 1])
-                nc.sync.dma_start(out_rows[:, tiles[0] : tiles[-1] + 1, lo:hi], result[:])
+                    if one_by_one:
+                        nc.sync.dma_start(out_rows[:, u, lo:hi], result[:, u, :])
+                if not one_by_one:
+                    nc.sync.dma_start(out_rows[:, tiles[0] : tiles[-1] + 1, lo:hi], result[:])
 
         def finish_early(q):
             lo, hi = x_spans[q]
@@ -291,9 +295,11 @@ def tile_list_silu_kernel(tc, xT, wgt, wt_words, wt_scales, c, wx_words, wx_scal
         def gather_upper(lo, hi):
             gather(3, lo, hi, last_plane[:, lo - HALF : hi - HALF])
 
-        for q in (0, 1):
-            gather(3, *x_spans[q], last_pairs[q][:, 1, :])
-            nc.scalar.copy(woven(x_parts[q])[:, :, 2:4, :], planar(last_pairs[q]))
+        for lo, hi in ((0, SUB), (SUB, CHUNK), (CHUNK, HALF)):
+            q, at = divmod(lo, CHUNK)
+            pair = last_pairs[q][:, :, at : at + hi - lo]
+            gather(3, lo, hi, pair[:, 1, :])
+            nc.scalar.copy(woven(x_parts[q][:, at * PACK : (at + hi - lo) * PACK])[:, :, 2:4, :], planar(pair))
         weave_c(EARLY_TIERS)
         gather_upper(HALF + SUB, J - SUB)
         finish_early(0)

@@ -18,22 +18,13 @@ ACT = mybir.ActivationFunctionType
 
 P = 128
 PACK = 4
-SUB = 128
-BANK = 512
+PIECE = 128
+CHUNK = 256
+CHUNKS = J // CHUNK
 N_TILES = N // P
 HALF = J // 2
-C_WIDTHS = (256, 256, 256, 256)
-EARLY_LOADS = 3
-T_WIDTHS = (128, 128, 128, 128, 256, 256)
-EARLY_TIERS = 5
-EARLY = 768
-VECTOR_TIERS = (0, 2)
-X_WIDTHS = (256, 256, 256, 256)
-CHUNK = 256
-
-
-def spans(widths):
-    return [(sum(widths[:q]), sum(widths[: q + 1])) for q in range(len(widths))]
+QUADS = 4
+STARTS = (768, 0, 256, 512)
 
 
 def woven(ap):
@@ -46,289 +37,247 @@ def planar(ap):
 
 def tile_list_silu_kernel(tc, xT, wgt, wt_words, wt_scales, c, wx_words, wx_scales, b, offs, out):
     nc = tc.nc
-    c_spans = spans(C_WIDTHS)
-    t_spans = spans(T_WIDTHS)
-    x_spans = spans(X_WIDTHS)
     with ExitStack() as ctx:
         keep = ctx.enter_context(tc.tile_pool(name="keep", bufs=1))
         psum = ctx.enter_context(tc.psum_pool(name="psum", bufs=1))
 
         offsets = keep.tile([P, J // 16], U16, name="offsets")
-        c_f32 = [keep.tile([P, PACK, w], F32, name="c_f32", tag="rows_%d" % q, align_bytes=64) for q, w in enumerate(C_WIDTHS)]
+        c_f32 = [keep.tile([P, PACK, CHUNK], F32, name="c_f32", tag="rows_%d" % q, align_bytes=64) for q in range(CHUNKS)]
         planes = [keep.tile([P, T], F32, name="plane_%d" % t, align_bytes=64) for t in range(PACK)]
         wgt_sb = keep.tile([P, J], F32, name="wgt_sb", align_bytes=64)
         wt_codes = keep.tile([P, N * 4], U8, name="wt_codes", align_bytes=64)
         wx_codes = keep.tile([P, N * 2], U8, name="wx_codes", align_bytes=64)
-        w_planes = keep.tile([P, 2 * N], U8, name="w_planes", align_bytes=64)
-        wx_plane, wt_plane = w_planes[:, :N], w_planes[:, N:]
+        w_scales = keep.tile([P, 2 * N], U8, name="w_scales", align_bytes=64)
+        wx_plane, wt_plane = w_scales[:, :N], w_scales[:, N : 2 * N]
         distance = keep.tile([P, PACK * P], BF16, name="distance", align_bytes=64)
         eye_bf = keep.tile([P, PACK * PACK * P], BF16, name="eye_bf", tag="woven_c", align_bytes=64)
         eye_codes = keep.tile([P, PACK * P], U32, name="eye_codes", align_bytes=64)
         eye_plane = keep.tile([P, PACK * P], U8, name="eye_plane", align_bytes=64)
-        cq_codes = keep.tile([P, J], U32, name="cq_codes", align_bytes=64)
-        cq_plane = keep.tile([P, J], U8, name="cq_plane", align_bytes=64)
-        cr_codes = keep.tile([P, J], U32, name="cr_codes", align_bytes=64)
-        cr_plane = keep.tile([P, J], U8, name="cr_plane", align_bytes=64)
-        xq_codes = keep.tile([P, J], U32, name="xq_codes", align_bytes=64)
-        xq_plane = keep.tile([P, J], U8, name="xq_plane", align_bytes=64)
+        eye_f32 = keep.tile([P, P], F32, name="eye_f32", align_bytes=64)
+        bias_rows = keep.tile([P, P], F32, name="bias_rows", align_bytes=64)
+        bias = keep.tile([P, N_TILES], F32, name="bias", align_bytes=64)
+        codes = keep.tile([P, 3 * J], U32, name="codes", align_bytes=64)
+        scales = keep.tile([P, 3 * J], U8, name="scales", align_bytes=64)
+        first_at = (0, 256, 512, 768)
+        rest_at = (1024, 1280, 1536, 1792)
+        x_at = (2048, 2304, 2560, 2816)
         rest_bf = keep.tile([P, HALF * PACK], BF16, name="rest_bf", align_bytes=64)
+        late = keep.tile([P, 13 * CHUNK], U32, name="late", align_bytes=64)
+
+        def blocks(first, last, dtype):
+            return late[:, first * CHUNK : last * CHUNK].bitcast(dtype)
+
+        x_woven = blocks(5, 13, BF16)
+        first_pair = keep.tile([P, 2 * CHUNK], F32, name="first_pair", align_bytes=64)
+        held_rest = first_pair[:].bitcast(BF16)
+
+        def last_pair(q):
+            if q == 0:
+                return first_pair[:].rearrange("p (t c) -> p t c", t=2)
+            first = STARTS[q] // CHUNK
+            return blocks(first, first + 6, F32).rearrange("p (t c) -> p t c", t=2)[:, :, :CHUNK]
 
         nc.gpsimd.iota(distance[:], [[1, PACK * P]], base=0, channel_multiplier=-PACK, allow_small_or_imprecise_dtypes=True)
         last_slice = (PACK - 1) * PACK * P
         nc.scalar.activation(eye_bf[:, last_slice : last_slice + 2], distance[:, :2], ACT.Silu, scale=0.0)
-        nc.vector.memset(w_planes[:].bitcast(I32), 0)
-        bias_rows = keep.tile([P, P], F32, name="bias_rows", align_bytes=64)
+        nc.vector.memset(w_scales[:].bitcast(I32), 0)
         nc.vector.memset(bias_rows[:], 0.0)
         for t in range(PACK):
             skip = 2 if t == PACK - 1 else 0
             nc.vector.tensor_scalar(eye_bf[:, t * PACK * P + skip : (t + 1) * PACK * P], distance[:, skip:], float(t), None, ALU.is_equal)
-        eye_f32 = keep.tile([P, P], F32, name="eye_f32", align_bytes=64)
         nc.scalar.copy(eye_f32[:], eye_bf[:, 0 : PACK * P : PACK])
-        nc.vector.quantize_mx(out=eye_codes[:].bitcast(FP8X4), scales=eye_plane[:], in_=eye_bf[:, : PACK * PACK * P])
-        c_bf = keep.tile([P, J * PACK], BF16, name="c_bf", tag="woven_c", align_bytes=64)
-
-        x_lower = keep.tile([P, HALF * PACK], BF16, name="x_lower", align_bytes=64)
-        x_upper = keep.tile([P, (HALF + CHUNK) * PACK], BF16, name="x_upper", align_bytes=64)
-        second_pair = keep.tile([P, 2 * CHUNK], F32, name="second_pair", align_bytes=64)
-        shared = keep.tile([P, 22 * SUB], U32, name="shared", align_bytes=64)
-
-        def region(first, last, dtype):
-            return shared[:, first * SUB : last * SUB].bitcast(dtype)
-
-        def two_rows(first, second):
-            return region(first, 2 * second - first, F32).rearrange("p (t c) -> p t c", t=2)[:, :, :CHUNK]
-
-        late_c_bf = region(14, 18, BF16)
-        late_rest = x_upper[:, SUB * PACK : (SUB + CHUNK) * PACK]
-        third_halves = x_upper[:].rearrange("p (h c t) -> p h c t", h=2, t=PACK)[:, :, :SUB, :]
-        last_plane = region(11, 15, F32)
-        held_rest = second_pair[:].bitcast(BF16)
-        x_parts = [x_lower[:, : CHUNK * PACK], x_lower[:, CHUNK * PACK :], None, x_upper[:, HALF * PACK :]]
-        x_words = [xq_codes[:, lo:hi] for lo, hi in x_spans]
-        last_pairs = [two_rows(8, 10), second_pair[:].rearrange("p (t c) -> p t c", t=2), two_rows(0, 11), two_rows(4, 13)]
+        nc.vector.quantize_mx(out=eye_codes[:].bitcast(FP8X4), scales=eye_plane[:], in_=eye_bf[:])
+        c_bf = keep.tile([P, 3 * CHUNK * PACK], BF16, name="c_bf", tag="woven_c", align_bytes=64)
 
         c_rows = c.rearrange("(p t) j -> p t j", t=PACK)
         x_rows = xT.rearrange("(p t) n -> p t n", t=PACK)
-
-        def load_scales(plane, scales, quad):
-            nc.sync.dma_start(plane[32 * quad : 32 * quad + 4, :].bitcast(I32), scales[0, 4 * quad : 4 * quad + 4, :].bitcast(I32))
+        out_rows = out.rearrange("(u p) j -> p u j", p=P)
 
         def load_c(q):
-            lo, hi = c_spans[q]
-            nc.sync.dma_start(c_f32[q][:], c_rows[:, :, lo:hi])
+            nc.sync.dma_start(c_f32[q][:], c_rows[:, :, STARTS[q] : STARTS[q] + CHUNK])
 
-        for q in range(EARLY_LOADS - 1):
-            load_c(q)
+        def load_plane(t):
+            nc.sync.dma_start(planes[t][:], x_rows[:, t, :])
+
+        def load_scales(plane, rows):
+            for quad in range(QUADS):
+                nc.sync.dma_start(plane[32 * quad : 32 * quad + PACK, :].bitcast(I32), rows[0, PACK * quad : PACK * (quad + 1), :].bitcast(I32))
+
+        load_c(0)
+        load_c(1)
         nc.sync.dma_start(offsets[:], offs)
         nc.sync.dma_start(wgt_sb[:], wgt)
-        nc.sync.dma_start(planes[0][:], x_rows[:, 0, :])
-        load_c(EARLY_LOADS - 1)
+        load_plane(0)
+        load_plane(1)
+        load_c(2)
         nc.sync.dma_start(bias_rows[:N_TILES, :], b.rearrange("(u p) -> u p", p=P))
-        for quad in range(4):
-            load_scales(wt_plane, wt_scales, quad)
-        nc.sync.dma_start(planes[1][:], x_rows[:, 1, :])
-        nc.sync.dma_start(planes[2][:], x_rows[:, 2, :])
-        for quad in range(4):
-            load_scales(wx_plane, wx_scales, quad)
+        load_scales(wt_plane, wt_scales)
+        load_plane(2)
+        load_scales(wx_plane, wx_scales)
         nc.sync.dma_start(wx_codes[:].bitcast(I32), wx_words[0].bitcast(I32))
-        nc.sync.dma_start(planes[3][:], x_rows[:, 3, :])
-        for q in range(EARLY_LOADS, len(c_spans)):
-            load_c(q)
+        load_plane(3)
+        load_c(3)
         nc.sync.dma_start(wt_codes[:].bitcast(I32), wt_words[0].rearrange("p n t -> p (n t)").bitcast(I32))
 
-        def quantise(codes, plane, source, lo, hi):
-            nc.vector.quantize_mx(out=codes[:, lo:hi].bitcast(FP8X4), scales=plane[:, lo:hi], in_=source[:, lo * PACK : hi * PACK])
+        def quantise(at, source):
+            width = source.shape[1] // PACK
+            nc.vector.quantize_mx(out=codes[:, at : at + width].bitcast(FP8X4), scales=scales[:, at : at + width], in_=source)
+
+        def c_piece(s):
+            q, h = divmod(s, CHUNK // PIECE)
+            return c_f32[q][:, :, h * PIECE : (h + 1) * PIECE]
+
+        def piece_of(ap, g):
+            return ap[:, g * PIECE * PACK : (g + 1) * PIECE * PACK]
+
+        def first_column(s):
+            q, h = divmod(s, CHUNK // PIECE)
+            return first_at[q] + h * PIECE
 
         back = {}
 
-        def c_columns(lo, hi):
-            q = max(q for q, span in enumerate(c_spans) if span[0] <= lo)
-            return c_f32[q][:, :, lo - c_spans[q][0] : hi - c_spans[q][0]]
+        def bring_back(s):
+            at = first_column(s)
+            bank = psum.tile([P, PACK, PIECE], F32, name="back", tag="bank_%d" % (0, 1, 2, 3, 6, 7, 6, 7)[s])
+            for t in range(PACK):
+                nc.tensor.matmul_mx(
+                    out=bank[:, t, :],
+                    lhsT=eye_codes[:, t * P : (t + 1) * P].bitcast(FP8X4), lhsT_scale=eye_plane[:, t * P : (t + 1) * P],
+                    rhs=codes[:, at : at + PIECE].bitcast(FP8X4), rhs_scale=scales[:, at : at + PIECE], start=True, stop=True,
+                )
+            back[s] = bank
 
-        def tier_part(q):
-            lo, hi = t_spans[q]
-            if q in (0, 2):
-                return c_bf[:, : (hi - lo) * PACK]
-            if q == EARLY_TIERS:
-                return late_c_bf
-            return c_bf[:, lo * PACK : hi * PACK]
+        def residual(s, dst):
+            nc.vector.tensor_tensor(woven(dst), planar(c_piece(s)), planar(back[s][:]), ALU.subtract)
 
-        def weave_c(q):
-            lo, hi = t_spans[q]
-            copy = nc.vector.tensor_copy if q in VECTOR_TIERS else nc.scalar.copy
-            copy(woven(tier_part(q)), planar(c_columns(lo, hi)))
+        head_parts = [piece_of(c_bf, 0), piece_of(c_bf, 1), piece_of(c_bf, 0), piece_of(c_bf, 3)]
 
-        def first_tier(q):
-            lo, hi = t_spans[q]
-            nc.vector.quantize_mx(out=cq_codes[:, lo:hi].bitcast(FP8X4), scales=cq_plane[:, lo:hi], in_=tier_part(q))
-            for s0 in range(lo, hi, SUB):
-                bank = psum.tile([P, PACK, SUB], F32, name="back", tag="bank_%d" % (s0 % EARLY // SUB))
-                for t in range(PACK):
-                    nc.tensor.matmul_mx(
-                        out=bank[:, t, :],
-                        lhsT=eye_codes[:, t * P : (t + 1) * P].bitcast(FP8X4), lhsT_scale=eye_plane[:, t * P : (t + 1) * P],
-                        rhs=cq_codes[:, s0 : s0 + SUB].bitcast(FP8X4), rhs_scale=cq_plane[:, s0 : s0 + SUB], start=True, stop=True,
-                    )
-                back[s0] = bank
+        def weave_c(s):
+            copy = nc.vector.tensor_copy if s in (0, 2) else nc.scalar.copy
+            copy(woven(head_parts[s]), planar(c_piece(s)))
 
-        def residual(s0, dst=None):
-            dst = rest_bf[:, s0 * PACK : (s0 + SUB) * PACK] if dst is None else dst
-            nc.vector.tensor_tensor(
-                woven(dst),
-                planar(c_columns(s0, s0 + SUB)), planar(back[s0][:]), ALU.subtract,
-            )
+        def first_tier(s):
+            quantise(first_column(s), head_parts[s])
+            bring_back(s)
 
-        def wx_pass(dst, u, codes, plane, lo, hi, start, stop):
+        def wx_pass(dst, u, at, start, stop):
             n0 = u * P
             nc.tensor.matmul_mx(
                 out=dst, lhsT=wx_codes[:, 2 * n0 : 2 * (n0 + P)].bitcast(FP4X4), lhsT_scale=wx_plane[:, n0 : n0 + P],
-                rhs=codes[:, lo:hi].bitcast(FP8X4), rhs_scale=plane[:, lo:hi], start=start, stop=stop,
+                rhs=codes[:, at : at + CHUNK].bitcast(FP8X4), rhs_scale=scales[:, at : at + CHUNK], start=start, stop=stop,
             )
 
-        def wt_pass(dst, u, lo, hi, start, stop):
+        def wt_pass(dst, u, at, start, stop):
             n0 = u * P
             nc.tensor.matmul_mx(
                 out=dst, lhsT=wt_codes[:, 4 * n0 : 4 * (n0 + P)].bitcast(FP8X4), lhsT_scale=wt_plane[:, n0 : n0 + P],
-                rhs=x_words[lo // CHUNK].bitcast(FP8X4), rhs_scale=xq_plane[:, lo:hi], start=start, stop=stop,
+                rhs=codes[:, at : at + CHUNK].bitcast(FP8X4), rhs_scale=scales[:, at : at + CHUNK], start=start, stop=stop,
             )
 
-        for q in range(2):
-            weave_c(q)
-            first_tier(q)
+        def gather(t, lo, hi, dst):
+            nc.vector.tensor_tensor(dst, planes[t][:].indirect(offsets[:, lo // 16 : hi // 16]), wgt_sb[:, lo:hi], ALU.mult)
+
+        for s in range(2):
+            weave_c(s)
+            first_tier(s)
         weave_c(2)
         weave_c(3)
-        residual(0)
+        residual(0, piece_of(rest_bf, 0))
         first_tier(2)
         first_tier(3)
         for s in (1, 2, 3):
-            residual(s * SUB)
-        quantise(cr_codes, cr_plane, rest_bf, 0, 256)
+            residual(s, piece_of(rest_bf, s))
+        quantise(rest_at[0], rest_bf[:, : CHUNK * PACK])
 
         turned = psum.tile([P, P], F32, name="turned", tag="bank_3")
         nc.tensor.transpose(turned[:], bias_rows[:], eye_f32[:])
-        bias = keep.tile([P, N_TILES], F32, name="bias", align_bytes=64)
         nc.scalar.copy(bias[:], turned[:, :N_TILES])
 
-        def open_banks(lo, hi, first_bank, per_bank):
-            groups = []
-            for u0 in range(0, N_TILES, per_bank):
-                bank = psum.tile([P, per_bank, hi - lo], F32, name="sums", tag="bank_%d" % (first_bank + u0 // per_bank))
-                groups.append((bank, range(u0, u0 + per_bank)))
-            return groups
-
-        def tier_passes(groups, codes, plane, lo, hi, opens, closes):
-            for bank, tiles in groups:
-                for u in tiles:
-                    wx_pass(bank[:, u - tiles[0], :], u, codes, plane, lo, hi, opens and u == tiles[0], closes and u == tiles[-1])
-
-        def x_passes(groups, lo, hi, closes):
-            for bank, tiles in groups:
-                for u in tiles:
-                    wt_pass(bank[:, u - tiles[0], :], u, lo, hi, False, closes and u == tiles[-1])
-
         picked = keep.tile([P, 2 * J], F32, name="picked", tag="rows_1", align_bytes=64)
-        nc.vector.tensor_tensor(picked[:, :J], planes[0][:].indirect(offsets[:]), wgt_sb[:], ALU.mult)
-        weave_c(4)
-        first_tier(4)
-        quantise(cr_codes, cr_plane, rest_bf, 256, HALF)
+        gather(0, 0, J, picked[:, :J])
 
-        early_groups = []
+        def groups_of(first_bank):
+            return [
+                (psum.tile([P, 2, CHUNK], F32, name="sums", tag="bank_%d" % (first_bank + g)), range(2 * g, 2 * g + 2)) for g in range(2)
+            ]
 
-        def open_early(q):
-            lo, hi = x_spans[q]
-            groups = open_banks(lo, hi, 2 * q, 2)
-            for group in groups:
-                tier_passes([group], cq_codes, cq_plane, lo, hi, True, False)
-            for group in groups:
-                tier_passes([group], cr_codes, cr_plane, lo, hi, False, False)
-            early_groups.append(groups)
-
-        open_early(0)
-        open_early(1)
-        early_groups.append(open_banks(*x_spans[2], 6, 2))
-        tier_passes(early_groups[2], cq_codes, cq_plane, *x_spans[2], True, False)
-
-        def gather(t, lo, hi, dst=None):
-            dst = picked[:, t * J + lo : t * J + hi] if dst is None else dst
-            nc.vector.tensor_tensor(dst, planes[t][:].indirect(offsets[:, lo // 16 : hi // 16]), wgt_sb[:, lo:hi], ALU.mult)
-
-        def pair_rows(t, lo, hi):
-            return picked[:, t * J : (t + 2) * J].rearrange("p (t c) -> p t c", t=2)[:, :, lo:hi]
-
-        def quantise_x(q):
-            lo, hi = x_spans[q]
-            nc.vector.quantize_mx(out=x_words[q].bitcast(FP8X4), scales=xq_plane[:, lo:hi], in_=x_parts[q])
-
-        def gpsimd_round(dst, source):
-            nc.gpsimd.tensor_scalar(dst, source, 1.0, 0.0, ALU.mult, ALU.add)
-
-        out_rows = out.rearrange("(u p) j -> p u j", p=P)
-
-        gather(1, 0, HALF)
-        nc.scalar.copy(woven(x_lower[:])[:, :, 0:2, :], planar(pair_rows(0, 0, HALF)))
-        gather(1, HALF, J)
-        nc.scalar.copy(woven(x_upper[:, : SUB * PACK])[:, :, 0:2, :], planar(pair_rows(0, HALF, HALF + SUB)))
-        nc.scalar.copy(woven(x_upper[:, (SUB + CHUNK) * PACK :])[:, :, 0:2, :], planar(pair_rows(0, HALF + SUB, J)))
-        for q, span in enumerate(x_spans):
-            gather(2, *span, last_pairs[q][:, 0, :])
-
-        def store(groups, lo, hi):
+        def passes(one_pass, groups, at, opens, closes):
             for bank, tiles in groups:
-                result = keep.tile([P, len(tiles), hi - lo], F32, name="result_%d_%d" % (lo, tiles[0]))
-                one_by_one = lo == 0 and tiles[0] == 0
                 for u in tiles:
-                    nc.scalar.activation(result[:, u - tiles[0], :], bank[:, u - tiles[0], :], ACT.Silu, bias=bias[:, u : u + 1])
-                    if one_by_one:
-                        nc.sync.dma_start(out_rows[:, u, lo:hi], result[:, u, :])
-                if not one_by_one:
-                    nc.sync.dma_start(out_rows[:, tiles[0] : tiles[-1] + 1, lo:hi], result[:])
+                    one_pass(bank[:, u - tiles[0], :], u, at, opens and u == tiles[0], closes and u == tiles[-1])
 
-        def finish_early(q):
-            lo, hi = x_spans[q]
-            quantise_x(q)
-            x_passes(early_groups[q], lo, hi, True)
-            store(early_groups[q], lo, hi)
+        both = picked[:].rearrange("p (t c) -> p t c", t=2)
+        third_c = c_bf[:, 2 * CHUNK * PACK :]
+        nc.scalar.copy(woven(third_c), planar(c_f32[2][:]))
+        gather(1, 0, J, picked[:, J:])
+        quantise(first_at[2], third_c)
+        for s in (4, 5):
+            bring_back(s)
+        quantise(rest_at[1], rest_bf[:, CHUNK * PACK :])
+        nc.scalar.copy(woven(x_woven)[:, :, 0:2, :], planar(both))
+        gather(2, 0, STARTS[0], blocks(0, 3, F32))
+        gather(2, STARTS[0], J, last_pair(0)[:, 0, :])
 
-        def gpsimd_pair(q):
-            gpsimd_round(x_parts[q].rearrange("p (c t) -> p c t", t=PACK)[:, :, 2:4], last_pairs[q].rearrange("p t c -> p c t"))
+        groups = [groups_of(2 * q) for q in range(3)]
+        for q in range(3):
+            passes(wx_pass, groups[q], first_at[q], True, False)
+            if q < 2:
+                passes(wx_pass, groups[q], rest_at[q], False, False)
 
-        def gather_upper(lo, hi):
-            gather(3, lo, hi, last_plane[:, lo - HALF : hi - HALF])
+        def x_part(q):
+            return x_woven[:, STARTS[q] * PACK : (STARTS[q] + CHUNK) * PACK]
 
-        for lo, hi in ((0, SUB), (SUB, CHUNK), (CHUNK, HALF)):
-            q, at = divmod(lo, CHUNK)
-            pair = last_pairs[q][:, :, at : at + hi - lo]
-            gather(3, lo, hi, pair[:, 1, :])
-            nc.scalar.copy(woven(x_parts[q][:, at * PACK : (at + hi - lo) * PACK])[:, :, 2:4, :], planar(pair))
-        weave_c(EARLY_TIERS)
-        gather_upper(HALF + SUB, J - SUB)
-        finish_early(0)
-        gather_upper(HALF, HALF + SUB)
-        gpsimd_round(third_halves[:, :, :, 2:4], last_pairs[2].rearrange("p t (h c) -> p h c t", h=2))
-        for g, lo in enumerate(range(HALF, EARLY, SUB)):
-            residual(lo, held_rest[:, g * SUB * PACK : (g + 1) * SUB * PACK])
-        finish_early(1)
-        first_tier(EARLY_TIERS)
-        nc.vector.quantize_mx(out=cr_codes[:, HALF:EARLY].bitcast(FP8X4), scales=cr_plane[:, HALF:EARLY], in_=held_rest)
-        tier_passes(early_groups[2], cr_codes, cr_plane, *x_spans[2], False, False)
-        gather_upper(J - SUB, J)
-        for h, lo in enumerate(range(HALF, EARLY, SUB)):
-            nc.vector.quantize_mx(
-                out=xq_codes[:, lo : lo + SUB].bitcast(FP8X4), scales=xq_plane[:, lo : lo + SUB],
-                in_=third_halves[:, h, :, :].rearrange("p c t -> p (c t)"),
+        def store(bank, tiles, lo, one_by_one):
+            result = keep.tile([P, len(tiles), CHUNK], F32, name="result_%d_%d" % (lo, tiles[0]))
+            for u in tiles:
+                nc.scalar.activation(result[:, u - tiles[0], :], bank[:, u - tiles[0], :], ACT.Silu, bias=bias[:, u : u + 1])
+                if one_by_one:
+                    nc.sync.dma_start(out_rows[:, u, lo : lo + CHUNK], result[:, u - tiles[0], :])
+            if not one_by_one:
+                nc.sync.dma_start(out_rows[:, tiles[0] : tiles[-1] + 1, lo : lo + CHUNK], result[:])
+
+        def finish(q):
+            quantise(x_at[q], x_part(q))
+            passes(wt_pass, groups[q], x_at[q], False, True)
+            for bank, tiles in groups[q]:
+                store(bank, tiles, STARTS[q], q == 0 and tiles[0] == 0)
+
+        def last_gather(q):
+            gather(3, STARTS[q], STARTS[q] + CHUNK, last_pair(q)[:, 1, :])
+
+        def gpsimd_weave(q):
+            nc.gpsimd.tensor_scalar(
+                x_part(q).rearrange("p (c t) -> p c t", t=PACK)[:, :, 2:4], last_pair(q).rearrange("p t c -> p c t"), 1.0, 0.0, ALU.mult, ALU.add
             )
-        x_passes(early_groups[2], HALF, EARLY, True)
-        store(early_groups[2], HALF, EARLY)
-        gpsimd_pair(3)
-        for g, lo in enumerate(range(EARLY, J, SUB)):
-            residual(lo, late_rest[:, g * SUB * PACK : (g + 1) * SUB * PACK])
-        late_groups = [
-            (psum.tile([P, 1, CHUNK], F32, name="sums", tag="bank_%d" % bank), range(u, u + 1)) for u, bank in enumerate((2, 3, 0, 1))
+
+        for q in range(2):
+            last_gather(q)
+            nc.scalar.copy(woven(x_part(q))[:, :, 2:4, :], planar(last_pair(q)))
+        late_c = keep.tile([P, CHUNK * PACK], BF16, name="late_c", tag="rows_0", align_bytes=64)
+        nc.scalar.copy(woven(late_c[:]), planar(c_f32[3][:]))
+        last_gather(2)
+        gpsimd_weave(2)
+        finish(0)
+        for g in range(2):
+            residual(4 + g, piece_of(held_rest, g))
+        finish(1)
+        quantise(first_at[3], late_c[:])
+        for s in (6, 7):
+            bring_back(s)
+        quantise(rest_at[2], held_rest)
+        passes(wx_pass, groups[2], rest_at[2], False, False)
+        last_gather(3)
+        gpsimd_weave(3)
+        finish(2)
+        for g in range(2):
+            residual(6 + g, piece_of(rest_bf, g))
+        last_groups = [
+            (psum.tile([P, 1, CHUNK], F32, name="sums", tag="bank_%d" % bank), range(u, u + 1)) for u, bank in enumerate((2, 3, 6, 7))
         ]
-        tier_passes(late_groups, cq_codes, cq_plane, EARLY, J, True, False)
-        nc.vector.quantize_mx(out=cr_codes[:, EARLY:].bitcast(FP8X4), scales=cr_plane[:, EARLY:], in_=late_rest)
-        quantise_x(3)
-        for group in late_groups:
-            tier_passes([group], cr_codes, cr_plane, EARLY, J, False, False)
-            x_passes([group], EARLY, J, True)
-            store([group], EARLY, J)
+        passes(wx_pass, last_groups, first_at[3], True, False)
+        quantise(x_at[3], x_part(3))
+        quantise(rest_at[3], rest_bf[:, : CHUNK * PACK])
+        for group in last_groups:
+            passes(wt_pass, [group], x_at[3], False, False)
+            passes(wx_pass, [group], rest_at[3], False, True)
+            store(*group, STARTS[3], False)

@@ -24,6 +24,7 @@ CHUNKS = J // CHUNK
 N_TILES = N // P
 HALF = J // 2
 QUADS = 4
+SCALAR_SHARE = 192
 STARTS = (768, 0, 256, 512)
 
 
@@ -245,29 +246,31 @@ def tile_list_silu_kernel(tc, xT, wgt, wt_words, wt_scales, c, wx_words, wx_scal
         def last_gather(q):
             gather(3, STARTS[q], STARTS[q] + CHUNK, last_pair(q)[:, 1, :])
 
-        def gpsimd_weave(q):
-            nc.gpsimd.tensor_scalar(
-                x_part(q).rearrange("p (c t) -> p c t", t=PACK)[:, :, 2:4], last_pair(q).rearrange("p t c -> p c t"), 1.0, 0.0, ALU.mult, ALU.add
-            )
+        def gpsimd_weave(dst, pair):
+            nc.gpsimd.tensor_scalar(dst.rearrange("p (c t) -> p c t", t=PACK)[:, :, 2:4], pair.rearrange("p t c -> p c t"), 1.0, 0.0, ALU.mult, ALU.add)
 
-        for q in range(2):
-            last_gather(q)
-            nc.scalar.copy(woven(x_part(q))[:, :, 2:4, :], planar(last_pair(q)))
         late_c = keep.tile([P, CHUNK * PACK], BF16, name="late_c", tag="rows_0", align_bytes=64)
-        nc.scalar.copy(woven(late_c[:]), planar(c_f32[3][:]))
-        last_gather(2)
-        gpsimd_weave(2)
+
+        middle = blocks(0, 6, F32).rearrange("p (t c) -> p t c", t=2)
+        last_gather(0)
+        nc.scalar.copy(woven(x_part(0))[:, :, 2:4, :], planar(last_pair(0)))
+        gather(3, 0, PIECE, middle[:, 1, :PIECE])
+        nc.scalar.copy(woven(x_woven[:, : PIECE * PACK])[:, :, 2:4, :], planar(middle[:, :, :PIECE]))
+        gather(3, PIECE, HALF, middle[:, 1, PIECE:HALF])
+        gpsimd_weave(x_woven[:, PIECE * PACK : HALF * PACK], middle[:, :, PIECE:HALF])
+        nc.scalar.copy(woven(late_c[:, : SCALAR_SHARE * PACK]), planar(c_f32[3][:, :, :SCALAR_SHARE]))
         finish(0)
         for g in range(2):
             residual(4 + g, piece_of(held_rest, g))
+        nc.vector.tensor_copy(woven(late_c[:, SCALAR_SHARE * PACK :]), planar(c_f32[3][:, :, SCALAR_SHARE:]))
+        quantise(rest_at[2], held_rest)
         finish(1)
         quantise(first_at[3], late_c[:])
         for s in (6, 7):
             bring_back(s)
-        quantise(rest_at[2], held_rest)
         passes(wx_pass, groups[2], rest_at[2], False, False)
         last_gather(3)
-        gpsimd_weave(3)
+        gpsimd_weave(x_part(3), last_pair(3))
         finish(2)
         for g in range(2):
             residual(6 + g, piece_of(rest_bf, g))

@@ -50,7 +50,7 @@ def tile_list_silu_kernel(tc, xT, wgt, wt_words, wt_scales, c, wx_words, wx_scal
         wx_codes = keep.tile([P, N * 2], U8, name="wx_codes", align_bytes=64)
         w_scales = keep.tile([P, 2 * N], U8, name="w_scales", align_bytes=64)
         wx_plane, wt_plane = w_scales[:, :N], w_scales[:, N : 2 * N]
-        distance = keep.tile([P, PACK * P], BF16, name="distance", align_bytes=64)
+        distance = keep.tile([P, 2 * P], BF16, name="distance", align_bytes=64)
         eye_bf = keep.tile([P, PACK * PACK * P], BF16, name="eye_bf", tag="woven_c", align_bytes=64)
         eye_codes = keep.tile([P, PACK * P], U32, name="eye_codes", align_bytes=64)
         eye_plane = keep.tile([P, PACK * P], U8, name="eye_plane", align_bytes=64)
@@ -78,16 +78,16 @@ def tile_list_silu_kernel(tc, xT, wgt, wt_words, wt_scales, c, wx_words, wx_scal
             first = STARTS[q] // CHUNK
             return blocks(first, first + 6, F32).rearrange("p (t c) -> p t c", t=2)[:, :, :CHUNK]
 
-        nc.gpsimd.iota(distance[:], [[1, PACK * P]], base=0, channel_multiplier=-PACK, allow_small_or_imprecise_dtypes=True)
-        last_slice = (PACK - 1) * PACK * P
-        nc.scalar.activation(eye_bf[:, last_slice : last_slice + 2], distance[:, :2], ACT.Silu, scale=0.0)
+        nc.gpsimd.iota(distance[:], [[1, 2 * P]], base=P, channel_multiplier=-PACK, allow_small_or_imprecise_dtypes=True)
+        nc.scalar.activation(bias_rows[:], distance[:, :P], ACT.Silu, scale=0.0)
         nc.vector.memset(w_scales[:].bitcast(I32), 0)
-        nc.vector.memset(bias_rows[:], 0.0)
         for t in range(PACK):
-            skip = 2 if t == PACK - 1 else 0
-            nc.vector.tensor_scalar(eye_bf[:, t * PACK * P + skip : (t + 1) * PACK * P], distance[:, skip:], float(t), None, ALU.is_equal)
-        nc.scalar.copy(eye_f32[:], eye_bf[:, 0 : PACK * P : PACK])
+            for h in range(2):
+                at = (2 * t + h) * 2 * P
+                nc.vector.tensor_scalar(eye_bf[:, at : at + 2 * P], distance[:], float(P + t - 2 * P * h), None, ALU.is_equal)
         nc.vector.quantize_mx(out=eye_codes[:].bitcast(FP8X4), scales=eye_plane[:], in_=eye_bf[:])
+        for h in range(2):
+            nc.vector.tensor_scalar(eye_f32[:, h * P // 2 : (h + 1) * P // 2], distance[:, ::PACK], float(P - 2 * P * h), None, ALU.is_equal)
         c_bf = keep.tile([P, 3 * CHUNK * PACK], BF16, name="c_bf", tag="woven_c", align_bytes=64)
 
         c_rows = c.rearrange("(p t) j -> p t j", t=PACK)

@@ -24,8 +24,9 @@ CHUNKS = J // CHUNK
 N_TILES = N // P
 HALF = J // 2
 QUADS = 4
-SCALAR_SHARE = 192
-STARTS = (768, 0, 256, 512)
+STARTS = (0, 256, 512, 768)
+WGT_FIRST = 512
+TURNED_PIECES = (4, 5)
 
 
 def woven(ap):
@@ -43,7 +44,8 @@ def tile_list_silu_kernel(tc, xT, wgt, wt_words, wt_scales, c, wx_words, wx_scal
         psum = ctx.enter_context(tc.psum_pool(name="psum", bufs=1))
 
         offsets = keep.tile([P, J // 16], U16, name="offsets")
-        c_f32 = [keep.tile([P, PACK, CHUNK], F32, name="c_f32", tag="rows_%d" % q, align_bytes=64) for q in range(CHUNKS)]
+        c_f32 = [keep.tile([P, PACK, CHUNK], F32, name="c_f32", tag="rows_%d" % q, align_bytes=64) for q in range(CHUNKS - 1)]
+        c_late = [keep.tile([P, PACK, PIECE], F32, name="c_late_%d" % h, align_bytes=64) for h in range(2)]
         planes = [keep.tile([P, T], F32, name="plane_%d" % t, align_bytes=64) for t in range(PACK)]
         wgt_sb = keep.tile([P, J], F32, name="wgt_sb", align_bytes=64)
         wt_codes = keep.tile([P, N * 4], U8, name="wt_codes", align_bytes=64)
@@ -60,26 +62,24 @@ def tile_list_silu_kernel(tc, xT, wgt, wt_words, wt_scales, c, wx_words, wx_scal
         codes = keep.tile([P, 3 * J], U32, name="codes", align_bytes=64)
         scales = keep.tile([P, 3 * J], U8, name="scales", align_bytes=64)
         first_at = (0, 256, 512, 768)
-        rest_at = (1024, 1280, 1536, 1792)
-        x_at = (2048, 2304, 2560, 2816)
-        rest_bf = keep.tile([P, HALF * PACK], BF16, name="rest_bf", align_bytes=64)
-        late = keep.tile([P, 13 * CHUNK], U32, name="late", align_bytes=64)
+        rest_at = (1024, 1280, 2304, 1536)
+        x_at = (1792, 2048, 2560, 2816)
+        rest_bf = keep.tile([P, 2 * CHUNK * PACK], BF16, name="rest_bf", align_bytes=64)
+        late = keep.tile([P, 17 * CHUNK], U32, name="late", align_bytes=64)
 
         def blocks(first, last, dtype):
             return late[:, first * CHUNK : last * CHUNK].bitcast(dtype)
 
-        x_woven = blocks(5, 13, BF16)
-        first_pair = keep.tile([P, 2 * CHUNK], F32, name="first_pair", align_bytes=64)
-        held_rest = first_pair[:].bitcast(BF16)
+        x_halves = (blocks(7, 11, BF16), blocks(13, 17, BF16))
+        turned_rest = blocks(11, 13, BF16)
 
         def last_pair(q):
-            if q == 0:
-                return first_pair[:].rearrange("p (t c) -> p t c", t=2)
-            first = STARTS[q] // CHUNK
-            return blocks(first, first + 6, F32).rearrange("p (t c) -> p t c", t=2)[:, :, :CHUNK]
+            step = 3 if q == 3 else 4
+            return blocks(q, q + 2 * step, F32).rearrange("p (t c) -> p t c", t=2)[:, :, :CHUNK]
 
         nc.gpsimd.iota(distance[:], [[1, 2 * P]], base=P, channel_multiplier=-PACK, allow_small_or_imprecise_dtypes=True)
-        nc.scalar.activation(bias_rows[:], distance[:, :P], ACT.Silu, scale=0.0)
+        nc.vector.memset(bias_rows[: P // 2, :], 0.0)
+        nc.scalar.activation(bias_rows[P // 2 :, :], distance[P // 2 :, :P], ACT.Silu, scale=0.0)
         nc.vector.memset(w_scales[:].bitcast(I32), 0)
         for t in range(PACK):
             for h in range(2):
@@ -107,18 +107,20 @@ def tile_list_silu_kernel(tc, xT, wgt, wt_words, wt_scales, c, wx_words, wx_scal
         load_c(0)
         load_c(1)
         nc.sync.dma_start(offsets[:], offs)
-        nc.sync.dma_start(wgt_sb[:], wgt)
-        load_plane(0)
-        load_plane(1)
+        nc.sync.dma_start(wgt_sb[:, :WGT_FIRST], wgt[:, :WGT_FIRST])
         load_c(2)
+        load_plane(0)
+        nc.sync.dma_start(wgt_sb[:, WGT_FIRST:], wgt[:, WGT_FIRST:])
         nc.sync.dma_start(bias_rows[:N_TILES, :], b.rearrange("(u p) -> u p", p=P))
         load_scales(wt_plane, wt_scales)
+        load_plane(1)
         load_plane(2)
         load_scales(wx_plane, wx_scales)
         nc.sync.dma_start(wx_codes[:].bitcast(I32), wx_words[0].bitcast(I32))
         load_plane(3)
-        load_c(3)
+        nc.sync.dma_start(c_late[0][:], c_rows[:, :, STARTS[3] : STARTS[3] + PIECE])
         nc.sync.dma_start(wt_codes[:].bitcast(I32), wt_words[0].rearrange("p n t -> p (n t)").bitcast(I32))
+        nc.sync.dma_start(c_late[1][:], c_rows[:, :, STARTS[3] + PIECE :])
 
         def quantise(at, source):
             width = source.shape[1] // PACK
@@ -126,7 +128,7 @@ def tile_list_silu_kernel(tc, xT, wgt, wt_words, wt_scales, c, wx_words, wx_scal
 
         def c_piece(s):
             q, h = divmod(s, CHUNK // PIECE)
-            return c_f32[q][:, :, h * PIECE : (h + 1) * PIECE]
+            return c_late[h][:] if q == 3 else c_f32[q][:, :, h * PIECE : (h + 1) * PIECE]
 
         def piece_of(ap, g):
             return ap[:, g * PIECE * PACK : (g + 1) * PIECE * PACK]
@@ -139,7 +141,7 @@ def tile_list_silu_kernel(tc, xT, wgt, wt_words, wt_scales, c, wx_words, wx_scal
 
         def bring_back(s):
             at = first_column(s)
-            bank = psum.tile([P, PACK, PIECE], F32, name="back", tag="bank_%d" % (0, 1, 2, 3, 6, 7, 6, 7)[s])
+            bank = psum.tile([P, PACK, PIECE], F32, name="back", tag="bank_%d" % s)
             for t in range(PACK):
                 nc.tensor.matmul_mx(
                     out=bank[:, t, :],
@@ -151,7 +153,7 @@ def tile_list_silu_kernel(tc, xT, wgt, wt_words, wt_scales, c, wx_words, wx_scal
         def residual(s, dst):
             nc.vector.tensor_tensor(woven(dst), planar(c_piece(s)), planar(back[s][:]), ALU.subtract)
 
-        head_parts = [piece_of(c_bf, 0), piece_of(c_bf, 1), piece_of(c_bf, 0), piece_of(c_bf, 3)]
+        head_parts = [piece_of(c_bf, 0), piece_of(c_bf, 1), piece_of(c_bf, 0), piece_of(c_bf, 3), piece_of(c_bf, 4), piece_of(c_bf, 5)]
 
         def weave_c(s):
             copy = nc.vector.tensor_copy if s in (0, 2) else nc.scalar.copy
@@ -178,29 +180,52 @@ def tile_list_silu_kernel(tc, xT, wgt, wt_words, wt_scales, c, wx_words, wx_scal
         def gather(t, lo, hi, dst):
             nc.vector.tensor_tensor(dst, planes[t][:].indirect(offsets[:, lo // 16 : hi // 16]), wgt_sb[:, lo:hi], ALU.mult)
 
+        def turned_sum(s, bank, pairs):
+            minus = keep.tile([P, PACK, PIECE], F32, name="minus_%d" % s, align_bytes=64)
+            nc.scalar.mul(minus[:], back[s][:], -1.0)
+            total = psum.tile([P, PACK, P], F32, name="total", tag="bank_%d" % bank)
+            for t in range(PACK):
+                nc.tensor.matmul(total[:, t, :], c_piece(s)[:, t, :], eye_f32[:], start=t == 0, stop=False, is_transpose=True)
+            for t in range(PACK):
+                nc.tensor.matmul(total[:, t, :], minus[:, t, :], eye_f32[:], start=False, stop=t == PACK - 1, is_transpose=True)
+            nc.scalar.copy(pairs.bitcast(BF16).rearrange("j u (p e) -> j u p e", e=2), total[:].rearrange("j (u e) p -> j u p e", e=2))
+
+        def turn_back(bank, pairs, dst):
+            words = psum.tile([P, 2, PIECE], F32, name="words", tag="bank_%d" % bank)
+            for u in range(2):
+                nc.tensor.transpose(words[:, u, :], pairs[:, u, :], eye_f32[:])
+            nc.scalar.copy(dst.bitcast(F32).rearrange("p (j u) -> p j u", u=2), words[:].rearrange("p u j -> p j u"))
+
         for s in range(2):
             weave_c(s)
             first_tier(s)
-        weave_c(2)
-        weave_c(3)
+        for s in range(2, 6):
+            weave_c(s)
         residual(0, piece_of(rest_bf, 0))
         first_tier(2)
         first_tier(3)
-        for s in (1, 2, 3):
-            residual(s, piece_of(rest_bf, s))
-        quantise(rest_at[0], rest_bf[:, : CHUNK * PACK])
-
-        turned = psum.tile([P, P], F32, name="turned", tag="bank_3")
+        residual(1, piece_of(rest_bf, 1))
+        residual(2, piece_of(rest_bf, 2))
+        first_tier(4)
+        residual(3, piece_of(rest_bf, 3))
+        first_tier(5)
+        quantise(rest_at[0], rest_bf[:])
+        first_pairs = keep.tile([P, 2, P], F32, name="first_pairs", align_bytes=64)
+        pairs = (first_pairs[:], blocks(10, 16, F32).rearrange("j (u w) -> j u w", u=2)[:, :, :P])
+        for g, s in enumerate(TURNED_PIECES):
+            turned_sum(s, 1 + 2 * g, pairs[g])
+        for g in range(2):
+            turn_back(6 + g, pairs[g], piece_of(turned_rest, g))
+        turned = psum.tile([P, P], F32, name="turned", tag="bank_6")
         nc.tensor.transpose(turned[:], bias_rows[:], eye_f32[:])
         nc.scalar.copy(bias[:], turned[:, :N_TILES])
 
-        picked = keep.tile([P, 2 * J], F32, name="picked", tag="rows_1", align_bytes=64)
-        gather(0, 0, J, picked[:, :J])
+        picked = keep.tile([P, 2 * J], F32, name="picked", tag="woven_c", align_bytes=64)
+        gather(0, 0, WGT_FIRST, picked[:, :WGT_FIRST])
+        gather(0, WGT_FIRST, J, picked[:, WGT_FIRST:J])
 
-        def groups_of(first_bank):
-            return [
-                (psum.tile([P, 2, CHUNK], F32, name="sums", tag="bank_%d" % (first_bank + g)), range(2 * g, 2 * g + 2)) for g in range(2)
-            ]
+        def groups_of(banks):
+            return [(psum.tile([P, 2, CHUNK], F32, name="sums", tag="bank_%d" % bank), range(2 * g, 2 * g + 2)) for g, bank in enumerate(banks)]
 
         def passes(one_pass, groups, at, opens, closes):
             for bank, tiles in groups:
@@ -208,25 +233,19 @@ def tile_list_silu_kernel(tc, xT, wgt, wt_words, wt_scales, c, wx_words, wx_scal
                     one_pass(bank[:, u - tiles[0], :], u, at, opens and u == tiles[0], closes and u == tiles[-1])
 
         both = picked[:].rearrange("p (t c) -> p t c", t=2)
-        third_c = c_bf[:, 2 * CHUNK * PACK :]
-        nc.scalar.copy(woven(third_c), planar(c_f32[2][:]))
-        gather(1, 0, J, picked[:, J:])
-        quantise(first_at[2], third_c)
-        for s in (4, 5):
-            bring_back(s)
-        quantise(rest_at[1], rest_bf[:, CHUNK * PACK :])
-        nc.scalar.copy(woven(x_woven)[:, :, 0:2, :], planar(both))
-        gather(2, 0, STARTS[0], blocks(0, 3, F32))
-        gather(2, STARTS[0], J, last_pair(0)[:, 0, :])
+        for h, lo in enumerate((0, HALF)):
+            gather(1, lo, lo + HALF, picked[:, J + lo : J + lo + HALF])
+            nc.scalar.copy(woven(x_halves[h])[:, :, 0:2, :], planar(both[:, :, lo : lo + HALF]))
+        gather(2, 0, J, blocks(0, 4, F32))
 
-        groups = [groups_of(2 * q) for q in range(3)]
+        groups = [groups_of(bank) for bank in ((0, 2), (4, 5), (1, 3))]
         for q in range(3):
             passes(wx_pass, groups[q], first_at[q], True, False)
             if q < 2:
                 passes(wx_pass, groups[q], rest_at[q], False, False)
 
         def x_part(q):
-            return x_woven[:, STARTS[q] * PACK : (STARTS[q] + CHUNK) * PACK]
+            return x_halves[q // 2][:, q % 2 * CHUNK * PACK : (q % 2 + 1) * CHUNK * PACK]
 
         def store(bank, tiles, lo, one_by_one):
             result = keep.tile([P, len(tiles), CHUNK], F32, name="result_%d_%d" % (lo, tiles[0]))
@@ -238,8 +257,14 @@ def tile_list_silu_kernel(tc, xT, wgt, wt_words, wt_scales, c, wx_words, wx_scal
                 nc.sync.dma_start(out_rows[:, tiles[0] : tiles[-1] + 1, lo : lo + CHUNK], result[:])
 
         def finish(q):
-            quantise(x_at[q], x_part(q))
-            passes(wt_pass, groups[q], x_at[q], False, True)
+            if q == 2:
+                quantise(rest_at[q], blocks(11, 15, BF16))
+            else:
+                quantise(x_at[q], x_part(q))
+            for group in groups[q]:
+                if q == 2:
+                    passes(wx_pass, [group], rest_at[q], False, False)
+                passes(wt_pass, [group], x_at[q], False, True)
             for bank, tiles in groups[q]:
                 store(bank, tiles, STARTS[q], q == 0 and tiles[0] == 0)
 
@@ -251,31 +276,29 @@ def tile_list_silu_kernel(tc, xT, wgt, wt_words, wt_scales, c, wx_words, wx_scal
 
         late_c = keep.tile([P, CHUNK * PACK], BF16, name="late_c", tag="rows_0", align_bytes=64)
 
-        middle = blocks(0, 6, F32).rearrange("p (t c) -> p t c", t=2)
+        def weave_pair(copy, q):
+            copy(woven(x_part(q))[:, :, 2:4, :], planar(last_pair(q)))
+
         last_gather(0)
-        nc.scalar.copy(woven(x_part(0))[:, :, 2:4, :], planar(last_pair(0)))
-        gather(3, 0, PIECE, middle[:, 1, :PIECE])
-        nc.scalar.copy(woven(x_woven[:, : PIECE * PACK])[:, :, 2:4, :], planar(middle[:, :, :PIECE]))
-        gather(3, PIECE, HALF, middle[:, 1, PIECE:HALF])
-        gpsimd_weave(x_woven[:, PIECE * PACK : HALF * PACK], middle[:, :, PIECE:HALF])
-        nc.scalar.copy(woven(late_c[:, : SCALAR_SHARE * PACK]), planar(c_f32[3][:, :, :SCALAR_SHARE]))
+        weave_pair(nc.scalar.copy, 0)
+        nc.scalar.copy(woven(piece_of(late_c, 0)), planar(c_piece(6)))
+        last_gather(1)
+        last_gather(2)
+        weave_pair(nc.scalar.copy, 2)
+        weave_pair(nc.vector.tensor_copy, 1)
         finish(0)
-        for g in range(2):
-            residual(4 + g, piece_of(held_rest, g))
-        nc.vector.tensor_copy(woven(late_c[:, SCALAR_SHARE * PACK :]), planar(c_f32[3][:, :, SCALAR_SHARE:]))
-        quantise(rest_at[2], held_rest)
         finish(1)
-        quantise(first_at[3], late_c[:])
+        nc.vector.tensor_copy(woven(piece_of(late_c, 1)), planar(c_piece(7)))
         for s in (6, 7):
+            quantise(first_column(s), piece_of(late_c, s - 6))
             bring_back(s)
-        passes(wx_pass, groups[2], rest_at[2], False, False)
         last_gather(3)
         gpsimd_weave(x_part(3), last_pair(3))
         finish(2)
         for g in range(2):
             residual(6 + g, piece_of(rest_bf, g))
         last_groups = [
-            (psum.tile([P, 1, CHUNK], F32, name="sums", tag="bank_%d" % bank), range(u, u + 1)) for u, bank in enumerate((2, 3, 6, 7))
+            (psum.tile([P, 1, CHUNK], F32, name="sums", tag="bank_%d" % bank), range(u, u + 1)) for u, bank in enumerate((4, 5, 6, 7))
         ]
         passes(wx_pass, last_groups, first_at[3], True, False)
         quantise(x_at[3], x_part(3))

from contextlib import ExitStack

import concourse.mybir as mybir

K, L, N, T, J = 512, 512, 512, 2048, 1024
FLOPS = 2 * N * J * (K + 2 * L) + 2 * L * L * J

F32 = mybir.dt.float32
BF16 = mybir.dt.bfloat16
I32 = mybir.dt.int32
U32 = mybir.dt.uint32
U16 = mybir.dt.uint16
U8 = mybir.dt.uint8
FP8X4 = mybir.dt.float8_e4m3fn_x4
FP4X4 = mybir.dt.float4_e2m1fn_x4
ALU = mybir.AluOpType
ACT = mybir.ActivationFunctionType

P = 128
PACK = 4
PIECE = 128
CHUNK = 256
CHUNKS = J // CHUNK
N_TILES = N // P
HALF = J // 2
QUADS = 4
STARTS = (0, 256, 512, 768)
WGT_FIRST = 512
TURNED_PIECES = (4, 5)


def woven(ap):
    return ap.rearrange("p (c i t) -> p c t i", i=2, t=PACK)


def planar(ap):
    return ap.rearrange("p t (c i) -> p c t i", i=2)


def tile_list_silu_kernel(tc, xT, wgt, wt_words, wt_scales, c, wx_words, wx_scales, b, offs, out):
    nc = tc.nc
    with ExitStack() as ctx:
        keep = ctx.enter_context(tc.tile_pool(name="keep", bufs=1))
        psum = ctx.enter_context(tc.psum_pool(name="psum", bufs=1))

        offsets = keep.tile([P, J // 16], U16, name="offsets")
        c_f32 = [keep.tile([P, PACK, CHUNK], F32, name="c_f32", tag="rows_%d" % q, align_bytes=64) for q in range(CHUNKS - 1)]
        c_late = [keep.tile([P, PACK, PIECE], F32, name="c_late_%d" % h, align_bytes=64) for h in range(2)]
        planes = [keep.tile([P, T], F32, name="plane_%d" % t, align_bytes=64) for t in range(PACK)]
        wgt_sb = keep.tile([P, J], F32, name="wgt_sb", align_bytes=64)
        wt_codes = keep.tile([P, N * 4], U8, name="wt_codes", align_bytes=64)
        wx_codes = keep.tile([P, N * 2], U8, name="wx_codes", align_bytes=64)
        w_scales = keep.tile([P, 2 * N], U8, name="w_scales", align_bytes=64)
        wx_plane, wt_plane = w_scales[:, :N], w_scales[:, N : 2 * N]
        distance = keep.tile([P, 2 * P], BF16, name="distance", align_bytes=64)
        eye_bf = keep.tile([P, PACK * PACK * P], BF16, name="eye_bf", tag="woven_c", align_bytes=64)
        eye_codes = keep.tile([P, PACK * P], U32, name="eye_codes", align_bytes=64)
        eye_plane = keep.tile([P, PACK * P], U8, name="eye_plane", align_bytes=64)
        eye_f32 = keep.tile([P, P], F32, name="eye_f32", align_bytes=64)
        bias_rows = keep.tile([P, P], F32, name="bias_rows", align_bytes=64)
        bias = keep.tile([P, N_TILES], F32, name="bias", align_bytes=64)
        codes = keep.tile([P, 3 * J], U32, name="codes", align_bytes=64)
        scales = keep.tile([P, 3 * J], U8, name="scales", align_bytes=64)
        first_at = (0, 256, 512, 768)
        rest_at = (1024, 1280, 2304, 1536)
        x_at = (1792, 2048, 2560, 2816)
        rest_bf = keep.tile([P, 2 * CHUNK * PACK], BF16, name="rest_bf", align_bytes=64)
        late = keep.tile([P, 17 * CHUNK], U32, name="late", align_bytes=64)

        def blocks(first, last, dtype):
            return late[:, first * CHUNK : last * CHUNK].bitcast(dtype)

        x_halves = (blocks(7, 11, BF16), blocks(13, 17, BF16))
        turned_rest = blocks(11, 13, BF16)

        def last_pair(q):
            step = 3 if q == 3 else 4
            return blocks(q, q + 2 * step, F32).rearrange("p (t c) -> p t c", t=2)[:, :, :CHUNK]

        nc.gpsimd.iota(distance[:], [[1, 2 * P]], base=P, channel_multiplier=-PACK, allow_small_or_imprecise_dtypes=True)
        nc.vector.memset(bias_rows[: P // 2, :], 0.0)
        nc.scalar.activation(bias_rows[P // 2 :, :], distance[P // 2 :, :P], ACT.Silu, scale=0.0)
        nc.vector.memset(w_scales[:].bitcast(I32), 0)
        for t in range(PACK):
            for h in range(2):
                at = (2 * t + h) * 2 * P
                nc.vector.tensor_scalar(eye_bf[:, at : at + 2 * P], distance[:], float(P + t - 2 * P * h), None, ALU.is_equal)
        nc.vector.quantize_mx(out=eye_codes[:].bitcast(FP8X4), scales=eye_plane[:], in_=eye_bf[:])
        for h in range(2):
            nc.vector.tensor_scalar(eye_f32[:, h * P // 2 : (h + 1) * P // 2], distance[:, ::PACK], float(P - 2 * P * h), None, ALU.is_equal)
        c_bf = keep.tile([P, 3 * CHUNK * PACK], BF16, name="c_bf", tag="woven_c", align_bytes=64)

        c_rows = c.rearrange("(p t) j -> p t j", t=PACK)
        x_rows = xT.rearrange("(p t) n -> p t n", t=PACK)
        out_rows = out.rearrange("(u p) j -> p u j", p=P)

        def load_c(q):
            nc.sync.dma_start(c_f32[q][:], c_rows[:, :, STARTS[q] : STARTS[q] + CHUNK])

        def load_plane(t):
            nc.sync.dma_start(planes[t][:], x_rows[:, t, :])

        def load_scales(plane, rows):
            for quad in range(QUADS):
                nc.sync.dma_start(plane[32 * quad : 32 * quad + PACK, :].bitcast(I32), rows[0, PACK * quad : PACK * (quad + 1), :].bitcast(I32))

        load_c(0)
        load_c(1)
        nc.sync.dma_start(offsets[:], offs)
        nc.sync.dma_start(wgt_sb[:, :WGT_FIRST], wgt[:, :WGT_FIRST])
        load_c(2)
        load_plane(0)
        nc.sync.dma_start(wgt_sb[:, WGT_FIRST:], wgt[:, WGT_FIRST:])
        nc.sync.dma_start(bias_rows[:N_TILES, :], b.rearrange("(u p) -> u p", p=P))
        load_scales(wt_plane, wt_scales)
        load_plane(1)
        load_plane(2)
        load_scales(wx_plane, wx_scales)
        nc.sync.dma_start(wx_codes[:].bitcast(I32), wx_words[0].bitcast(I32))
        load_plane(3)
        nc.sync.dma_start(c_late[0][:], c_rows[:, :, STARTS[3] : STARTS[3] + PIECE])
        nc.sync.dma_start(wt_codes[:].bitcast(I32), wt_words[0].rearrange("p n t -> p (n t)").bitcast(I32))
        nc.sync.dma_start(c_late[1][:], c_rows[:, :, STARTS[3] + PIECE :])

        def quantise(at, source):
            width = source.shape[1] // PACK
            nc.vector.quantize_mx(out=codes[:, at : at + width].bitcast(FP8X4), scales=scales[:, at : at + width], in_=source)

        def c_piece(s):
            q, h = divmod(s, CHUNK // PIECE)
            return c_late[h][:] if q == 3 else c_f32[q][:, :, h * PIECE : (h + 1) * PIECE]

        def piece_of(ap, g):
            return ap[:, g * PIECE * PACK : (g + 1) * PIECE * PACK]

        def first_column(s):
            q, h = divmod(s, CHUNK // PIECE)
            return first_at[q] + h * PIECE

        back = {}

        def bring_back(s):
            at = first_column(s)
            bank = psum.tile([P, PACK, PIECE], F32, name="back", tag="bank_%d" % s)
            for t in range(PACK):
                nc.tensor.matmul_mx(
                    out=bank[:, t, :],
                    lhsT=eye_codes[:, t * P : (t + 1) * P].bitcast(FP8X4), lhsT_scale=eye_plane[:, t * P : (t + 1) * P],
                    rhs=codes[:, at : at + PIECE].bitcast(FP8X4), rhs_scale=scales[:, at : at + PIECE], start=True, stop=True,
                )
            back[s] = bank

        def residual(s, dst):
            nc.vector.tensor_tensor(woven(dst), planar(c_piece(s)), planar(back[s][:]), ALU.subtract)

        head_parts = [piece_of(c_bf, 0), piece_of(c_bf, 1), piece_of(c_bf, 0), piece_of(c_bf, 3), piece_of(c_bf, 4), piece_of(c_bf, 5)]

        def weave_c(s):
            copy = nc.vector.tensor_copy if s in (0, 2) else nc.scalar.copy
            copy(woven(head_parts[s]), planar(c_piece(s)))

        def first_tier(s):
            quantise(first_column(s), head_parts[s])
            bring_back(s)

        def wx_pass(dst, u, at, start, stop):
            n0 = u * P
            nc.tensor.matmul_mx(
                out=dst, lhsT=wx_codes[:, 2 * n0 : 2 * (n0 + P)].bitcast(FP4X4), lhsT_scale=wx_plane[:, n0 : n0 + P],
                rhs=codes[:, at : at + CHUNK].bitcast(FP8X4), rhs_scale=scales[:, at : at + CHUNK], start=start, stop=stop,
            )

        def wt_pass(dst, u, at, start, stop):
            n0 = u * P
            nc.tensor.matmul_mx(
                out=dst, lhsT=wt_codes[:, 4 * n0 : 4 * (n0 + P)].bitcast(FP8X4), lhsT_scale=wt_plane[:, n0 : n0 + P],
                rhs=codes[:, at : at + CHUNK].bitcast(FP8X4), rhs_scale=scales[:, at : at + CHUNK], start=start, stop=stop,
            )

        def gather(t, lo, hi, dst):
            nc.vector.tensor_tensor(dst, planes[t][:].indirect(offsets[:, lo // 16 : hi // 16]), wgt_sb[:, lo:hi], ALU.mult)

        def turned_sum(s, bank, pairs):
            minus = keep.tile([P, PACK, PIECE], F32, name="minus_%d" % s, align_bytes=64)
            nc.scalar.mul(minus[:], back[s][:], -1.0)
            total = psum.tile([P, PACK, P], F32, name="total", tag="bank_%d" % bank)
            for t in range(PACK):
                nc.tensor.matmul(total[:, t, :], c_piece(s)[:, t, :], eye_f32[:], start=t == 0, stop=False, is_transpose=True)
            for t in range(PACK):
                nc.tensor.matmul(total[:, t, :], minus[:, t, :], eye_f32[:], start=False, stop=t == PACK - 1, is_transpose=True)
            nc.scalar.copy(pairs.bitcast(BF16).rearrange("j u (p e) -> j u p e", e=2), total[:].rearrange("j (u e) p -> j u p e", e=2))

        def turn_back(bank, pairs, dst):
            words = psum.tile([P, 2, PIECE], F32, name="words", tag="bank_%d" % bank)
            for u in range(2):
                nc.tensor.transpose(words[:, u, :], pairs[:, u, :], eye_f32[:])
            nc.scalar.copy(dst.bitcast(F32).rearrange("p (j u) -> p j u", u=2), words[:].rearrange("p u j -> p j u"))

        for s in range(2):
            weave_c(s)
            first_tier(s)
        for s in range(2, 6):
            weave_c(s)
        residual(0, piece_of(rest_bf, 0))
        first_tier(2)
        first_tier(3)
        residual(1, piece_of(rest_bf, 1))
        residual(2, piece_of(rest_bf, 2))
        first_tier(4)
        residual(3, piece_of(rest_bf, 3))
        first_tier(5)
        quantise(rest_at[0], rest_bf[:])
        first_pairs = keep.tile([P, 2, P], F32, name="first_pairs", align_bytes=64)
        pairs = (first_pairs[:], blocks(10, 16, F32).rearrange("j (u w) -> j u w", u=2)[:, :, :P])
        for g, s in enumerate(TURNED_PIECES):
            turned_sum(s, 1 + 2 * g, pairs[g])
        for g in range(2):
            turn_back(6 + g, pairs[g], piece_of(turned_rest, g))
        turned = psum.tile([P, P], F32, name="turned", tag="bank_6")
        nc.tensor.transpose(turned[:], bias_rows[:], eye_f32[:])
        nc.scalar.copy(bias[:], turned[:, :N_TILES])

        picked = keep.tile([P, 2 * J], F32, name="picked", tag="woven_c", align_bytes=64)
        gather(0, 0, WGT_FIRST, picked[:, :WGT_FIRST])
        gather(0, WGT_FIRST, J, picked[:, WGT_FIRST:J])

        def groups_of(banks):
            return [(psum.tile([P, 2, CHUNK], F32, name="sums", tag="bank_%d" % bank), range(2 * g, 2 * g + 2)) for g, bank in enumerate(banks)]

        def passes(one_pass, groups, at, opens, closes):
            for bank, tiles in groups:
                for u in tiles:
                    one_pass(bank[:, u - tiles[0], :], u, at, opens and u == tiles[0], closes and u == tiles[-1])

        both = picked[:].rearrange("p (t c) -> p t c", t=2)
        for h, lo in enumerate((0, HALF)):
            gather(1, lo, lo + HALF, picked[:, J + lo : J + lo + HALF])
            nc.scalar.copy(woven(x_halves[h])[:, :, 0:2, :], planar(both[:, :, lo : lo + HALF]))
        gather(2, 0, J, blocks(0, 4, F32))

        groups = [groups_of(bank) for bank in ((0, 2), (4, 5), (1, 3))]
        for q in range(3):
            passes(wx_pass, groups[q], first_at[q], True, False)
            if q < 2:
                passes(wx_pass, groups[q], rest_at[q], False, False)

        def x_part(q):
            return x_halves[q // 2][:, q % 2 * CHUNK * PACK : (q % 2 + 1) * CHUNK * PACK]

        def store(bank, tiles, lo, one_by_one):
            result = keep.tile([P, len(tiles), CHUNK], F32, name="result_%d_%d" % (lo, tiles[0]))
            for u in tiles:
                nc.scalar.activation(result[:, u - tiles[0], :], bank[:, u - tiles[0], :], ACT.Silu, bias=bias[:, u : u + 1])
                if one_by_one:
                    nc.sync.dma_start(out_rows[:, u, lo : lo + CHUNK], result[:, u - tiles[0], :])
            if not one_by_one:
                nc.sync.dma_start(out_rows[:, tiles[0] : tiles[-1] + 1, lo : lo + CHUNK], result[:])

        def finish(q):
            if q == 2:
                quantise(rest_at[q], blocks(11, 15, BF16))
            else:
                quantise(x_at[q], x_part(q))
            for group in groups[q]:
                if q == 2:
                    passes(wx_pass, [group], rest_at[q], False, False)
                passes(wt_pass, [group], x_at[q], False, True)
            for bank, tiles in groups[q]:
                store(bank, tiles, STARTS[q], q == 0 and tiles[0] == 0)

        def last_gather(q):
            gather(3, STARTS[q], STARTS[q] + CHUNK, last_pair(q)[:, 1, :])

        def gpsimd_weave(dst, pair):
            nc.gpsimd.tensor_scalar(dst.rearrange("p (c t) -> p c t", t=PACK)[:, :, 2:4], pair.rearrange("p t c -> p c t"), 1.0, 0.0, ALU.mult, ALU.add)

        late_c = keep.tile([P, CHUNK * PACK], BF16, name="late_c", tag="rows_0", align_bytes=64)

        def weave_pair(copy, q):
            copy(woven(x_part(q))[:, :, 2:4, :], planar(last_pair(q)))

        last_gather(0)
        weave_pair(nc.scalar.copy, 0)
        nc.scalar.copy(woven(piece_of(late_c, 0)), planar(c_piece(6)))
        last_gather(1)
        last_gather(2)
        weave_pair(nc.scalar.copy, 2)
        weave_pair(nc.vector.tensor_copy, 1)
        finish(0)
        finish(1)
        nc.vector.tensor_copy(woven(piece_of(late_c, 1)), planar(c_piece(7)))
        for s in (6, 7):
            quantise(first_column(s), piece_of(late_c, s - 6))
            bring_back(s)
        last_gather(3)
        gpsimd_weave(x_part(3), last_pair(3))
        finish(2)
        for g in range(2):
            residual(6 + g, piece_of(rest_bf, g))
        last_groups = [
            (psum.tile([P, 1, CHUNK], F32, name="sums", tag="bank_%d" % bank), range(u, u + 1)) for u, bank in enumerate((4, 5, 6, 7))
        ]
        passes(wx_pass, last_groups, first_at[3], True, False)
        quantise(x_at[3], x_part(3))
        quantise(rest_at[3], rest_bf[:, : CHUNK * PACK])
        for group in last_groups:
            passes(wt_pass, [group], x_at[3], False, False)
            passes(wx_pass, [group], rest_at[3], False, True)
            store(*group, STARTS[3], False)
